import numpy as np, ml_dtypes
CORES = [35,38,43,46]
N = 4
import mx_ref
BF = ml_dtypes.bfloat16
def gentries(a):
    return np.ascontiguousarray(a.reshape(8, 16, -1).transpose(0, 2, 1)).reshape(8, -1)
def gtable(e):
    e = np.asarray(e); return np.ascontiguousarray(e.reshape(8, -1, 16).transpose(0, 2, 1)).reshape(128, -1).astype(np.int32)
def gcols(t, e):
    v = np.concatenate([t.reshape(8, 16, -1, 4), np.zeros((8, 16, 1, 4), BF)], axis=2)
    return np.ascontiguousarray(np.stack([v[g][:, e[g]] for g in range(8)])).reshape(128, -1)
def tile(rs):
    return np.stack(rs, axis=2).reshape(128, -1).astype(BF)
def pick(q, e):
    c = np.concatenate([q[0].reshape(128, -1, 4), np.zeros((128, 1, 4), np.uint8)], axis=1); s = np.concatenate([q[1], np.ones((16, 1), np.uint8)], axis=1)
    return (np.ascontiguousarray(c[:, e].reshape(128, -1)), np.ascontiguousarray(s[:, e]))
def join(*qs):
    return (np.concatenate([q[0] for q in qs], axis=1), np.concatenate([q[1] for q in qs], axis=1))
def put(q, e, v):
    c, s = q[0].reshape(128, -1, 4).copy(), q[1].copy(); c[:, e] = v[0].reshape(128, -1, 4); s[:, e] = v[1]
    return (c.reshape(128, -1), s)
def pk(c, s):
    return (np.ascontiguousarray(c), mx_ref.live(s))
def emit(q):
    return q[0], q[1]
def packed(v, rng):
    q = [mx_ref.quantize(np.ascontiguousarray(v[r])) for r in range(N)]
    return np.stack([a for a, b in q]), np.stack([mx_ref.plane(b, rng) for a, b in q])
def values_of_codes():
    e, c = np.zeros((128, 128, 4), np.float32), np.zeros((128, 2, 4), np.uint8)
    e[np.arange(128), np.arange(128), 0] = 1
    c[:127, :, 0] = np.arange(256).reshape(2, 128).T[:127]
    return mx_ref.matmul(mx_ref.quantize(e.reshape(128, 512).astype(BF)), (c.reshape(128, 8), np.full((16, 2), 127, np.uint8))).T.reshape(-1).astype(np.float64)
CODE_VALUE, SCALE_VALUE = values_of_codes(), 2.0 ** (np.arange(256) - 127.0)
def decode(q):
    return (CODE_VALUE[q[0]].reshape(16, 8, -1, 4) * SCALE_VALUE[q[1]][:, None, :, None] + 0.0).reshape(128, -1).astype(np.float32)
def f(rng, *shape):
    return mx_ref.flush((rng.standard_normal(shape, dtype=np.float32) * np.exp2(rng.integers(-2, 3, shape[:-1] + (1,)))).astype(BF))
def wide(rng, *shape, cols=0):
    v = rng.standard_normal(shape, dtype=np.float32) * np.exp2(rng.integers(-12, 13, shape)).astype(np.float32)
    if cols: v *= np.repeat(np.exp2(rng.integers(-cols, cols + 1, shape[:-2] + (1, shape[-1] // 4))) * (rng.random(shape[:-2] + (1, shape[-1] // 4)) > 0.0625), 4, axis=-1).astype(np.float32)
    return mx_ref.flush(v.astype(BF))
C, M, R = 384, 160, 3
SH = (N, 8, 2, C, 4)
def numbers_of(rng):
    return {"x": np.array(f(rng, N, 128, 4 * C)), "u": np.array(f(rng, N, 128, 512)), "v": np.array(f(rng, N, 128, 512))}
def lists_of(e, c, a):
    return {"al": np.stack([gtable(e[r]) for r in range(N)]), "nx": np.stack([gtable((512 * c + a)[r].reshape(8, 8 * C)) for r in range(N)])}
def lists(rng):
    return lists_of(rng.integers(0, C, (N, 8, C)), rng.integers(0, 5, SH), rng.integers(0, C, SH))
def layers(rng, still=0):
    w = np.array(f(rng, N, 128, 2048)).reshape(N, 8, 16, 4, 8, 16, 4)
    w[:, :, :still] = 0
    w[:, :, :, :, :, :still] = 0
    return w
def weights(rng, w):
    c, s = packed(np.ascontiguousarray(w).reshape(N, 128, 2048), rng)
    return {"wc": c, "ws": s}
def setup_inputs(rng):
    return {**numbers_of(rng), **lists(rng), **weights(rng, layers(rng))}
def setup_inputs_near(rng):
    d = numbers_of(rng)
    x = d["x"].reshape(N, 8, 16, C, 4)
    u = d["u"].reshape(N, 128, 128, 4)
    o = rng.permutation(N) % 2
    x[:, :, :8] = 0
    u[:, :, ::16] = 0
    u[:, :, 1::16] = 0
    for r in range(N):
        k = 2.0 ** -30 if o[r] == 0 else 1.0
        s = rng.integers(-1, 2, (8, 2, C)) * k
        for g in rng.permutation(8)[:4]: s[g, :, rng.integers(C)] = 2.0 ** 14 * rng.choice([-1.0, 1.0], 2)
        x[r, :, :2, :, 0] = s.astype(np.float32).astype(BF)
        t = np.where(s[:, 0] == 0, rng.integers(-1, 2, (8, C)), 0) * k
        x[r, :, 2, :, 0] = (1.125 * t).astype(np.float32).astype(BF)
        x[r, :, 3, :, 0] = (-t).astype(np.float32).astype(BF)
        for h in [0, 16, 32, 48, 64, 80, 96, 112, 1, 17]:
            u[r, h, h, 0] = k
            u[r, h - h % 16 + 2, h, 0] = 1.125 * k
            u[r, h - h % 16 + 3, h, 0] = 1.25 * k
    return {"x": x.reshape(N, 128, 4 * C), "u": u.reshape(N, 128, 512), "v": d["v"], **lists(rng), **weights(rng, layers(rng, 8))}
def setup_inputs_chain(rng):
    d = numbers_of(rng)
    e = rng.permutation(N)
    c = rng.integers(0, 5, SH)
    i = np.arange(4)
    c[e[0]] = rng.integers(1, 5, SH[1:])
    c[e[1]] = 0
    c[e[2]] = np.where(np.arange(8)[:, None] <= 2 * i, i + 1, 0)[:, None, None, :]
    c[e[3]][:, 0] = 0
    c[e[3]][:, 1] = rng.integers(1, 5, (8, C, 4))
    return {**d, **lists_of(rng.integers(0, C, (N, 8, C)), c, rng.integers(0, C, SH)), **weights(rng, layers(rng))}
def setup_inputs_twice(rng):
    d = numbers_of(rng)
    s = 2.0 ** -rng.integers(8, 15, (N, 16, C, 32)) * (1.125 + 0.25 * rng.integers(0, 4, (N, 16, C, 32)))
    s[:, :, :, 4] = 2.0 ** -rng.integers(8, 12, (N, 16, C)) * (1.125 + 0.25 * rng.integers(0, 4, (N, 16, C)))
    np.put_along_axis(s, rng.integers(8, 32, (N, 16, C, 1)), 1.96875, axis=3)
    s = s * rng.choice([-1.0, 1.0], s.shape)
    s[:, :, :, 0] = 0.125 * s[:, :, :, 4]
    s = s * np.exp2(rng.integers(10, 13, (N, 16, C, 1)))
    x = np.ascontiguousarray(s.reshape(N, 16, C, 8, 4).transpose(0, 1, 3, 2, 4)).reshape(N, 128, 4 * C)
    u = d["u"].reshape(N, 128, 128, 4)
    u[:, :, ::16] = 0
    for h in range(0, 128, 16):
        u[:, h, h, 0] = 1.0
        u[:, h + 1, h, 0] = -0.125
    w = np.array(mx_ref.flush((layers(rng).astype(np.float32) * np.float32(2.0 ** -12)).astype(BF))).reshape(N, 128, 4, 128, 4)
    i = np.arange(128)
    for b in range(4): w[:, i, b, i, b] = -1.0
    return {"x": x.astype(np.float32).astype(BF), "u": u.reshape(N, 128, 512), "v": d["v"], **lists(rng), **weights(rng, w)}
def setup_inputs_ends(rng):
    d = numbers_of(rng)
    e = rng.permutation(N)
    x = d["x"].reshape(N, 8, 16, C, 4)
    u = d["u"].reshape(N, 128, 128, 4)
    v = d["v"].reshape(N, 128, 128, 4)
    t = np.clip(rng.integers(-C, 2 * C, (N, 8, C)), 0, C - 1)
    c = 4 * rng.integers(0, 2, SH)
    a = np.clip(rng.integers(-C, 2 * C, SH), 0, C - 1)
    t[e[0]], c[e[0]], a[e[0]] = C - 1, 4, C - 1
    t[e[1]], c[e[1]], a[e[1]] = 0, 0, 0
    u[:, :, ::16] = 0
    u[:, :, 1::16] = 0
    for i in range(N):
        r = e[i]
        s = rng.integers(-1, 2, (8, C)) * 1.0
        s[rng.permutation(8)[:2]] = rng.choice([-1.0, 1.0], (2, 1))
        s = s * (2.0 ** -30 if i % 2 else 2.0 ** 14)
        x[r, :, :8] = s[:, None, :, None].astype(np.float32).astype(BF)
        for h in [0, 16, 32, 48, 64, 80, 96, 112, 1, 17]: u[r, h - h % 16:h - h % 16 + 8, h] = 2.0 ** -30 if i % 2 else 2.0 ** 30
    x[e[0]] = (2.0 ** 14 * rng.choice([-1.0, 1.0], (C, 1))).astype(np.float32).astype(BF)
    u[e[0]] = (2.0 ** 30 * rng.choice([-1.0, 1.0], (128, 1))).astype(np.float32).astype(BF)
    v[e[0]] = (2.0 ** 30 * rng.choice([-1.0, 1.0], (128, 1))).astype(np.float32).astype(BF)
    w = layers(rng, 8)
    w[e[0]][:, 8:, :, :, 8:] = 8
    w[e[1]] = 0
    v = (np.where(v < 0, -1.0, 1.0) * np.where(rng.permutation(N) % 2, 2.0 ** -30, 2.0 ** 30)[:, None, None, None]).astype(np.float32).astype(BF)
    return {"x": x.reshape(N, 128, 4 * C), "u": u.reshape(N, 128, 512), "v": v.reshape(N, 128, 512), **lists_of(t, c, a), **weights(rng, w)}
def setup_inputs_spread(rng):
    d = setup_inputs(rng)
    d["x"] = mx_ref.flush((wide(rng, N, 128, 4 * C, cols=6).astype(np.float32) * np.float32(2.0 ** -7)).astype(BF))
    return d
def check_inputs(d):
    b = []
    for k, most in (("x", 2.0 ** 14), ("u", 2.0 ** 30), ("v", 2.0 ** 30)):
        a = np.abs(d[k].astype(np.float32))
        if not (np.isfinite(a).all() and ((a == 0) | (a >= 2.0 ** -30) & (a <= most)).all()): b.append("a value of " + k)
    if not ((d["al"] >= 0) & (d["al"] < C)).all(): b.append("an entry of al")
    if not ((d["nx"] >= 0) & (d["nx"] < 2560) & (d["nx"] % 512 < C)).all(): b.append("an entry of nx")
    none, least, most = [emit(mx_ref.quantize(np.full((128, 16), k, np.float32).astype(BF)))[1][0, 0] for k in (0.0, 2.0 ** -30, 2.0 ** 30)]
    for r in range(N):
        if ((d["wc"][r] == 0x7F) | (d["wc"][r] == 0xFF)).any(): b.append("wc: a code that is no number")
        s = mx_ref.live(d["ws"][r])
        if ((s != none) & ((s < least) | (s > most))).any(): b.append("ws: a scale out of range")
        w = np.abs(decode(pk(d["wc"][r], d["ws"][r])).astype(np.float64)).reshape(128, 512, 4)
        if not (np.sum(w, axis=(0, 2)) <= 2048).all(): b.append("a column of W adds up to more than 2048")
    return b
def reference(x, u, v, al, nx, wc, ws):
    qu = [mx_ref.quantize(u[r]) for r in range(N)]
    lay = [pk(wc[r], ws[r]) for r in range(N)]
    now = [x[r] for r in range(N)]
    ad = np.stack([gentries(al[r]) for r in range(N)])
    follow = [gentries(nx[r]) for r in range(N)]
    for t in range(R):
        made = []
        for r in range(N):
            q = mx_ref.quantize(now[r])
            s = mx_ref.matmul(qu[r], q)
            edge = 2 * (s[1] > 0) + (s[17] > 0)
            on = np.ones(C, bool)
            for g in range(8):
                bit = s[16 * g][ad[r, g]] > 0
                n = follow[r][g][4 * C * bit + 4 * ad[r, g] + edge]
                ad[r, g] = np.where(on, n % 512, ad[r, g])
                on = on & (n >= 512)
                edge = np.where(on, n // 512 - 1, 0)
            made.append(mx_ref.quantize(gcols(decode(q).astype(BF), ad[r])))
        ad[:, :, C - M:] = np.roll(ad[:, :, C - M:], 1, axis=0)
        for r in range(N):
            q = join(pick(made[r], np.arange(C - M)), pick(made[r - 1], np.arange(C - M, C)))
            own = decode(q)
            now[r] = tile([mx_ref.matmul(pick(lay[r], np.arange(128 * b, 128 * b + 128)), q) * np.float32(0.015625) + own[:, b::4] for b in range(4)])
    y, oa = np.zeros((N, 128, C), np.float32), np.zeros((N, 8, C), np.float32)
    oc, osc = np.zeros((N, 128, 4 * C), np.uint8), np.zeros((N, 16, C), np.uint8)
    for r in range(N):
        q = mx_ref.quantize(now[r])
        y[r] = mx_ref.matmul(mx_ref.quantize(v[r]), q)
        oa[r] = ad[r]
        oc[r], osc[r] = emit(q)
    return {"y": y, "oa": oa, "oc": oc, "osc": osc}

@@ -1,0 +1,470 @@
+from concourse.mybir import dt, AluOpType, ActivationFunctionType
+
+CODES = "float8_e4m3fn_x4"
+C, NO, NR, ROUNDS = 384, 224, 160, 3
+PARTS = ((0, NO), (NO, C))
+Q2 = (0, 4, 8, 12)
+EVEN0, ODD0 = 15, 3
+NCH = 28
+A_ROW = 9
+EDGE_ROWS = (4, 6)
+
+_F = "float32"
+SCRATCH = {
+    "NX": ("sbuf", [128, 192], "int32"), "CI": ("sbuf", [128, 192], "int32"), "NI": ("sbuf", [128, 192], "int32"),
+    "NT": ("sbuf", [128, 192], "int32"), "ND": ("sbuf", [128, 192], _F), "AT": ("sbuf", [128, 48], _F), "NF": ("sbuf", [128, 192], _F),
+    "U4": ("sbuf", [128, 192], _F), "UU": ("sbuf", [128, 192], _F), "UT": ("sbuf", [128, 192], _F), "V2": ("sbuf", [128, 192], _F),
+    "V4": ("sbuf", [128, 192], _F), "SE": ("sbuf", [128, 192], _F), "SO": ("sbuf", [128, 192], _F), "FE": ("sbuf", [128, 192], _F),
+    "FD": ("sbuf", [128, 192], _F), "HE": ("sbuf", [128, 192], _F), "HO": ("sbuf", [128, 192], _F),
+    "ZZ": ("sbuf", [128, 16 * NCH], _F), "AW": ("sbuf", [128, C], _F), "M9": ("sbuf", [128, 1], _F), "SC": ("sbuf", [128, 1], _F),
+    "TAB": ("sbuf", [128, 768], _F), "D0": ("sbuf", [128, 768], _F), "D1": ("sbuf", [128, 768], _F),
+    "TW": ("sbuf", [128, 776], _F), "RO": ("sbuf", [128, 256], _F), "RR": ("sbuf", [128, 192], _F),
+    "EO": ("sbuf", [128, 256], "bfloat16"), "ER": ("sbuf", [128, 192], "bfloat16"),
+    "CH": ("sbuf", [128, 32 * NCH], _F), "CE": ("sbuf", [128, 32 * NCH], "bfloat16"),
+    "MA": ("sbuf", [128, NCH], _F), "MB": ("sbuf", [128, NCH], _F),
+    "MM": ("sbuf", [128, 2 * NCH], "int32"), "YY": ("sbuf", [128, NCH], "int32"),
+    "GG": ("sbuf", [128, 16 * NCH], _F), "XS": ("sbuf", [128, 16 * NCH], _F),
+    "PI": ("sbuf", [128, 1], "int32"), "P15": ("sbuf", [128, 1], "int32"), "PU": ("sbuf", [128, 1], "int32"),
+    "P31": ("sbuf", [128, 1], "int32"), "PUF": ("sbuf", [128, 1], _F), "PLF": ("sbuf", [128, 1], _F), "PHF": ("sbuf", [128, 1], _F),
+    "E3": ("sbuf", [128, 1], "int32"), "E4": ("sbuf", [128, 1], "int32"), "KC": ("sbuf", [128, 4], _F),
+    "LP": ("sbuf", [128, 8], "int32"), "LPU": ("sbuf", [128, 8], "uint16"),
+    "ALI": ("sbuf", [128, 24], "int32"), "OAF": ("sbuf", [128, 32], _F), "OAT": ("sbuf", [128, 32], _F),
+    "L2O": ("sbuf", [128, 16], "uint16"), "L2R": ("sbuf", [128, 16], "uint16"),
+    "CT": ("sbuf", [128, 2048], "bfloat16"), "CTc": ("sbuf", [128, 512], CODES), "CTs": ("sbuf", [128, 512], "uint8"),
+    "UB": ("sbuf", [128, 512], "bfloat16"), "Uc": ("sbuf", [128, 128], CODES), "Us": ("sbuf", [128, 128], "uint8"),
+    "Pc": ("sbuf", [128, 128], CODES), "Ps": ("sbuf", [128, 128], "uint8"),
+    "VB": ("sbuf", [128, 512], "bfloat16"), "Vc": ("sbuf", [128, 128], CODES), "Vs": ("sbuf", [128, 128], "uint8"),
+    "Wc": ("sbuf", [128, 512], CODES), "Ws": ("sbuf", [128, 512], "uint8"),
+    "X": ("sbuf", [128, 4 * C], "bfloat16"), "FO": ("sbuf", [128, 4 * C], "bfloat16"), "FP": ("sbuf", [128, 4 * C], "bfloat16"),
+    "ZO": ("sbuf", [128, 4 * NO], "bfloat16"), "ZR": ("sbuf", [128, 4 * NR], "bfloat16"),
+    "ZOc": ("sbuf", [128, NO], CODES), "ZOs": ("sbuf", [128, NO], "uint8"),
+    "ZRc": ("sbuf", [128, NR], CODES), "ZRs": ("sbuf", [128, NR], "uint8"),
+    "Y": ("sbuf", [128, C], _F),
+}
+for _t in range(ROUNDS + 1):
+    SCRATCH["Qc%d" % _t] = ("sbuf", [128, C], CODES)
+    SCRATCH["Qs%d" % _t] = ("sbuf", [128, C], "uint8")
+for _t in range(ROUNDS):
+    SCRATCH["AL%d" % _t] = ("sbuf", [128, NCH], _F)
+    SCRATCH["Ac%d" % _t] = ("sbuf", [128, C], CODES)
+    SCRATCH["As%d" % _t] = ("sbuf", [128, C], "uint8")
+    SCRATCH["LO%d" % _t] = ("sbuf", [128, 16], "uint16")
+    SCRATCH["LS%d" % _t] = ("sbuf", [128, 12], "uint16")
+    SCRATCH["LR%d" % _t] = ("sbuf", [128, 12], "uint16")
+for _t in range(8):
+    SCRATCH["pb%d" % _t] = ("psum", [128, 512], _F)
+SEMAPHORES = ["cv", "cs", "ct", "cg", "sent"] + ["d%d" % i for i in range(48)] + ["q%d%d" % (t, h) for t in range(ROUNDS) for h in range(2)] + ["l%d" % t for t in range(ROUNDS)]
+
+
+def rank_program(g, core, T, topo):
+    rank = T.rank_of(core)
+    if rank is None:
+        return
+    n = len(T.cores)
+    nxt, prv = T.cores[(rank + 1) % n], T.cores[(rank - 1) % n]
+    n_in = len(topo.engines(prv, core))
+    rid, pid = topo.addr(nxt)[0], topo.addr(nxt)[1]
+    A = AluOpType
+    ACT = ActivationFunctionType
+    queue = {"v": g.vector, "s": g.scalar, "t": g.tensor, "g": g, "y": g.sync}
+    count, seen, hist, need_end = {}, {}, {}, {}
+
+    def view(name, c0, c1, step=1, p0=0, p1=128):
+        buf = T[name]
+        if step != 1:
+            ap = buf[p0:p1, c0:c1:step]
+        elif (p0, p1) == (0, 128):
+            ap = buf[:, c0:c1]
+        else:
+            ap = buf[p0:p1, c0:c1]
+        return (ap, (name, p0, p1, c0, c1, step))
+
+    def w(name, a=0, b=None, step=1):
+        return view(name, a, T[name].shape[1] if b is None else b, step)
+
+    def meet(a, b):
+        if a[1] >= b[2] or b[1] >= a[2] or a[3] >= b[4] or b[3] >= a[4]:
+            return False
+        return not (a[5] == b[5] and a[5] > 1 and (a[3] - b[3]) % a[5])
+
+    def waits(q, reads, writes):
+        need = {}
+        for kind, rects in (("r", reads), ("w", writes)):
+            for r in rects:
+                bank = r[0].startswith("pb")
+                for hk, hq, hsem, hval, hr in hist.get(r[0], []):
+                    if kind == "r" and hk == "r" and not (bank and hq != q):
+                        continue
+                    if kind == "w" and hq == q and q in "vstg" and not hsem.startswith("d") and (hk == "r" or q == "t"):
+                        continue
+                    if bank or meet(r, hr):
+                        need[hsem] = max(need.get(hsem, 0), hval)
+        for s in sorted(need):
+            if seen.get((q, s), 0) < need[s]:
+                queue[q].wait_ge(T.sem[s], need[s])
+                seen[(q, s)] = need[s]
+                need_end[s] = max(need_end.get(s, 0), need[s])
+
+    def note(q, sem, val, reads, writes):
+        for kind, rects in (("r", reads), ("w", writes)):
+            for r in rects:
+                lst = hist.setdefault(r[0], [])
+                if kind == "w" and r[5] == 1:
+                    lst[:] = [h for h in lst if not (h[4][1] >= r[1] and h[4][2] <= r[2] and h[4][3] >= r[3] and h[4][4] <= r[4] and h[1] == q)]
+                lst.append((kind, q, sem, val, r))
+
+    def op(q, call, reads, writes):
+        reads = [a[1] for a in reads]
+        writes = [a[1] for a in writes]
+        waits(q, reads, writes)
+        sem = "c" + q
+        count[sem] = count.get(sem, 0) + 1
+        call(queue[q]).then_inc(T.sem[sem], 1)
+        note(q, sem, count[sem], reads, writes)
+
+    n_dma = [0]
+
+    def dma(q, out, in_, reads=(), writes=()):
+        reads, writes = list(reads), list(writes)
+        waits(q, reads, writes)
+        sem = "d%d" % n_dma[0]
+        n_dma[0] += 1
+        count[sem] = 16
+        queue[q].dma_start(out, in_).then_inc(T.sem[sem], 16)
+        note(q, sem, 16, reads, writes)
+
+    def load(q, name, src, c0=0, c1=None):
+        v = w(name, c0, c1)
+        dma(q, v[0].bitcast(dt.uint8) if name == "Wc" else v[0], src, (), [v[1]])
+
+    def lands(name, c0, c1, sem, val):
+        hist.setdefault(name, []).append(("w", "far", sem, val, (name, 0, 128, c0, c1, 1)))
+        count[sem] = max(count.get(sem, 0), val)
+
+    def send(out, in_, rect, sem):
+        waits("g", [rect], [])
+        count["sent"] = count.get("sent", 0) + len(topo.engines(core, nxt))
+        g.remote_dma(out, in_, T.sem[sem], T.sem.sent, pid, rid, topo.mask(core, nxt))
+
+    def fill(ap, val):
+        op("v", lambda e: e.memset(ap[0], val), [], [ap])
+
+    def act(out, in_, func=ACT.Copy, scale=1.0, bias=0.0):
+        a = scale[0] if isinstance(scale, tuple) else scale
+        op("s", lambda e: e.activation(out[0], in_[0], func, bias=bias, scale=a), [in_] + ([scale] if isinstance(scale, tuple) else []), [out])
+
+    def copy(q, out, in_, scale=None):
+        if q == "s":
+            act(out, in_, ACT.Copy, 1.0 if scale is None else scale)
+        elif scale is None:
+            op(q, lambda e: e.tensor_copy(out[0], in_[0]), [in_], [out])
+        else:
+            ts(out, in_, scale, A.mult)
+
+    def ts(out, in_, s1, o1, s2=None, o2=None):
+        reads = [in_] + [s for s in (s1, s2) if isinstance(s, tuple)]
+        a1 = s1[0] if isinstance(s1, tuple) else s1
+        a2 = s2[0] if isinstance(s2, tuple) else s2
+        if o2 is None:
+            op("v", lambda e: e.tensor_scalar(out[0], in_[0], a1, None, o1), reads, [out])
+        else:
+            op("v", lambda e: e.tensor_scalar(out[0], in_[0], a1, a2, o1, o2), reads, [out])
+
+    def tt(out, a, b, o):
+        op("v", lambda e: e.tensor_tensor(out[0], a[0], b[0], o), [a, b], [out])
+
+    def scan(out, a, b):
+        op("v", lambda e: e.tensor_tensor_scan(out[0], a[0], b[0], 0.0, A.mult, A.add), [a, b], [out])
+
+    def turn(out, in_):
+        op("v", lambda e: e.transpose(out[0], in_[0]), [in_], [out])
+
+    def gather(q, out, win, off):
+        src = win[0].indirect(off[0])
+        if q == "s":
+            op(q, lambda e: e.activation(out[0], src, ACT.Copy), [win, off], [out])
+        else:
+            op(q, lambda e: e.tensor_copy(out[0], src), [win, off], [out])
+
+    def quant(c, s, tile, c0, c1, t0):
+        qc, qs, x = view(c, c0, c1), view(s, c0, c1), view(tile, t0, t0 + 4 * (c1 - c0))
+        op("v", lambda e: e.quantize_mx(qc[0], qs[0], x[0]), [x], [qc, qs])
+
+    bank = [0]
+
+    def product(pairs, rhs, c0, c1):
+        out = view("pb%d" % (bank[0] % 8), 0, c1 - c0)
+        bank[0] += 1
+        rc, rs = view(rhs[0], c0, c1), view(rhs[1], c0, c1)
+        for i, (c, s, a) in enumerate(pairs):
+            lc, ls = view(c, a, a + 128), view(s, a, a + 128)
+            first, last = i == 0, i == len(pairs) - 1
+            op("t", lambda e: e.matmul_mx(out[0], lc[0], ls[0], rc[0], rs[0], first, last), [lc, ls, rc, rs], [out])
+        return out
+
+    for t in range(ROUNDS):
+        for h, (c0, c1) in enumerate(PARTS):
+            for name in ("Ac%d" % t, "As%d" % t):
+                lands(name, c0, c1, "q%d%d" % (t, h if t else 0), 2 * n_in)
+        lands("LR%d" % t, 0, 12, "l%d" % t, n_in)
+
+    load("y", "NX", T.nx[:])
+    load("s", "X", T.x[:, 0:4 * NO], 0, 4 * NO)
+    load("y", "X", T.x[:, 4 * NO:4 * C], 4 * NO, 4 * C)
+    load("s", "UB", T.u[:])
+    load("y", "ALI", T.al[:])
+    load("y", "Wc", T.wc[:])
+    load("s", "Ws", T.ws[:])
+    load("y", "VB", T.v[:])
+
+    def iota(out, pattern, base, mult, loose=False):
+        if loose:
+            op("g", lambda e: e.iota(out[0], pattern, base, mult, allow_small_or_imprecise_dtypes=True), [], [out])
+        else:
+            op("g", lambda e: e.iota(out[0], pattern, base, mult), [], [out])
+    iota(w("PI"), [[1, 1]], 0, 1)
+    for b in range(2):
+        iota(w("AT", 24 * b, 24 * b + 24), [[128, 3], [0, 2], [1, 4]], 0, 0, True)
+    iota(w("LP"), [[16, 8]], 0, 0)
+    iota(w("AW"), [[1, C]], 0, 0, True)
+    iota(w("CT"), [[0, 2048]], 0, 0, True)
+    for b in range(4):
+        d = view("CT", 512 * b + b, 512 * b + 512, 4)
+        op("g", lambda e: e.affine_select(d[0], d[0], [[-1, 128]], A.not_equal, 64.0, 0, 1), [d], [d])
+    fill(w("ZZ"), 0.0)
+    ts(w("P15"), w("PI"), 15, A.bitwise_and)
+    ts(w("P31"), w("PI"), 31, A.bitwise_and)
+    ts(w("M9"), w("P15"), A_ROW, A.is_equal)
+    ts(w("PHF"), w("P31"), 4.0, A.mult)
+    for ph in range(4):
+        act(w("TAB", 192 * ph, 192 * ph + 96), w("AW", ph, C, 4), ACT.Copy, w("M9"))
+        copy("s", w("TAB", 192 * ph + 96, 192 * ph + 192), w("ZZ", 0, 96))
+    copy("s", w("D0", 0, 768, 2), w("ZZ", 0, 384))
+    for name in ("RO", "RR", "EO", "ER", "OAF"):
+        copy("s", w(name), w("ZZ", 0, T[name].shape[1]))
+    ts(w("AT"), w("AT"), w("PHF"), A.add)
+    for name, ratio in (("HE", 2.0), ("HO", 16.0)):
+        fill(w(name), ratio)
+        fill(w(name, 0, 192, 4), 0.0)
+    ts(w("SC"), w("P15"), 0, A.is_equal, 2.0 ** (ODD0 - EVEN0 - 3) - 1.0, A.mult)
+    ts(w("PU"), w("PI"), 4, A.logical_shift_right, 1, A.bitwise_and)
+    ts(w("E3"), w("P15"), EDGE_ROWS[0], A.is_equal)
+    ts(w("E4"), w("P15"), EDGE_ROWS[1], A.is_equal, 17, A.mult)
+    ts(w("SC"), w("SC"), 1.0, A.add)
+    copy("v", w("PUF"), w("PU"))
+    tt(w("LP", 0, 1), w("E3"), w("E4"), A.add)
+    ts(w("PLF"), w("PUF"), -1.0, A.mult, 1.0, A.add)
+    copy("v", w("LPU"), w("LP"))
+    for k in range(1, 4):
+        lo, up = 2.0 ** (EVEN0 + k), 2.0 ** (ODD0 + Q2[k])
+        ts(w("KC", k, k + 1), w("PUF"), up - lo, A.mult, lo, A.add)
+
+    ts(w("CI"), w("NX"), 9, A.logical_shift_right)
+    ts(w("U4"), w("CI"), 4.0, A.mult, -8.0, A.add)
+    tt(w("UU"), w("CI"), w("U4"), A.max)
+    turn(w("UT"), w("UU"))
+    act(w("V2"), w("UT"), ACT.Square)
+    act(w("V4"), w("V2"), ACT.Square)
+    scan(w("SO"), w("HO"), w("UT"))
+    ts(w("NI"), w("NX"), 511, A.bitwise_and)
+    turn(w("FD"), w("SO"))
+    turn(w("NT"), w("NI"))
+    scan(w("SE"), w("HE"), w("V4"))
+    tt(w("FD", 96, 192), w("FD", 96, 192), w("FD", 0, 96), A.subtract)
+    turn(w("FE"), w("SE"))
+    for e in range(3):
+        tt(w("ND", e, 192, 4), w("NT", e, 192, 4), w("NT", e + 1, 192, 4), A.subtract)
+    tt(w("ND", 3, 192, 4), w("NT", 3, 192, 4), w("AT"), A.subtract)
+    tt(w("FE", 96, 192), w("FE", 96, 192), w("FE", 0, 96), A.subtract)
+    turn(w("NF"), w("ND"))
+    tt(w("NF", 96, 192), w("NF", 96, 192), w("NF", 0, 96), A.subtract)
+
+    def to_row(q, name, e, r):
+        dma(q, T.TAB[r:128:16, :], T[name][e:128:4, :], [(name, 0, 128, 0, 192, 1), ("TAB", 16, 128, 0, 768, 1)], [("TAB", r, r + 1, 0, 768, 1)])
+    to_row("s", "FD", 3, 2)
+    to_row("y", "FE", 3, 0)
+    for e in range(4):
+        to_row("sysy"[e], "NF", e, 1 + 2 * e)
+    act(w("GG"), w("ZZ"), ACT.Identity, 1.0, 1.0)
+    copy("s", w("GG", 0, 16 * NCH, 8), w("ZZ", 0, 2 * NCH))
+    for t in range(ROUNDS):
+        copy("s", w("AL%d" % t, 27, 28), w("ZZ", 0, 1))
+
+    def send_x(t, c0, c1, h):
+        for a, b in (("Qc%d", "Ac%d"), ("Qs%d", "As%d")):
+            s, d = T[a % t][:, c0:c1], T[b % t][:, c0:c1]
+            if a == "Qc%d":
+                s, d = s.bitcast(dt.uint8), d.bitcast(dt.uint8)
+            send(d, s, (a % t, 0, 128, c0, c1, 1), "q%d%d" % (t, h))
+
+    def quant_x(t, h):
+        c0, c1 = PARTS[h]
+        quant("Qc%d" % t, "Qs%d" % t, "X", c0, c1, 4 * c0)
+
+    quant_x(0, 0)
+    quant_x(0, 1)
+    send_x(0, 0, C, 0)
+    quant("Uc", "Us", "UB", 0, 128, 0)
+    op("v", lambda e: e.tensor_copy(T.Pc[:, 0:128].bitcast(dt.uint32), T.Uc[:, 0:128].bitcast(dt.uint32).indirect(T.LPU[:, 0:8])), [w("Uc"), w("LPU")], [w("Pc")])
+    op("v", lambda e: e.tensor_copy(T.Ps[:, 0:128], T.Us[:, 0:128].indirect(T.LPU[:, 0:8])), [w("Us"), w("LPU")], [w("Ps")])
+    for name, o, a, b in (("L2O", 0, 0, 14), ("L2O", 14, 0, 2), ("L2R", 0, 14, 24), ("L2R", 10, 14, 16)):
+        ts(w(name, o, o + b - a), w("ALI", a, b), 2.0, A.mult)
+    ts(w("GG", 5, 16 * NCH, 16), w("ZZ", 0, NCH), w("PLF"), A.add)
+    ts(w("GG", 13, 16 * NCH, 16), w("ZZ", 0, NCH), w("PUF"), A.add)
+    quant("CTc", "CTs", "CT", 0, 512, 0)
+
+    def score(t, h):
+        c0, c1 = PARTS[h]
+        return product([("Pc", "Ps", 0)], ("Qc%d" % t, "Qs%d" % t), c0, c1)
+
+    def unpack(src, dst, h, qs):
+        c0, c1 = PARTS[h]
+        outs = [product([("CTc", "CTs", 128 * b)], src, c0, c1) for b in range(4)]
+        return [(qs[b], w(dst, C * b + c0, C * b + c1), outs[b]) for b in range(4)]
+
+    def take(jobs):
+        for q, out, ps in jobs:
+            copy(q, out, ps, 2.0 ** -6)
+
+    def bits(ps, h):
+        c0, c1 = PARTS[h]
+        ts(w("D1", 2 * c0, 2 * c1, 2), ps, 0.0, A.is_gt)
+
+    def choose(h):
+        c0, c1 = PARTS[h]
+        scan(w("TW", 7 + 2 * c0, 7 + 2 * c1), w("D0", 2 * c0, 2 * c1), w("D1", 2 * c0, 2 * c1))
+
+    def edges(h):
+        c0, c1 = PARTS[h]
+        m, name = c1 - c0, ("EO", "ER")[h]
+        for a, b, o in ((0, m, 0), (0, 16, m)):
+            copy("s", view(name, o, o + b - a, 1, 0, 32), view("D1", 2 * (c0 + a), 2 * (c0 + b), 2, 0, 32))
+
+    def turns(h, src, dst, p1):
+        m = (14, 10)[h]
+        first, second = ((0, 14), (8, 22))[h]
+        turn(view(dst, 32 * first, 32 * first + 16 * (m + 2), 1, 0, p1), view(src, 0, 16 * (m + 2), 1, 0, p1))
+        turn(view(dst, 32 * second, 32 * second + 32, 1, 0, p1), view(src, 16 * (m - 1), 16 * (m + 1), 1, 0, p1))
+        turn(view(dst, 32 * second + 32, 32 * second + 32 + 16 * m, 1, 0, p1), view(src, 16, 16 * (m + 1), 1, 0, p1))
+
+    def start():
+        p = lambda name, a, b, step: view(name, a, b, step, 0, 32)
+        act(p("MA", 0, NCH, 1), p("CE", EDGE_ROWS[0], 32 * NCH, 32), ACT.Identity, 3.0 * 2.0 ** EVEN0, 2.0 ** EVEN0)
+        act(p("MB", 0, NCH, 1), p("CE", EDGE_ROWS[1], 32 * NCH, 32), ACT.Identity, 1.0, 1.0)
+
+    def carries(t):
+        n2 = 2 * NCH
+        p = lambda name, a, b, step, q: view(name, a, b, step, 32 * q, 32 * q + 32)
+        masks = (sum(2 ** (ODD0 + k) for k in Q2), sum(2 ** (EVEN0 + k) for k in range(4)))
+        for s in range(7):
+            q, o = s // 2, s % 2
+            q2, o2 = (s + 1) // 2, (s + 1) % 2
+            tt(p("YY", 0, NCH, 1, q), p("CH", (0, 18)[o], 32 * NCH, 32, q), p("MM", o, n2, 2, q), A.mult)
+            ts(p("MM", o2, n2, 2, q2), p("YY", 0, NCH, 1, q), masks[o], A.bitwise_and)
+        for k in range(1, 4):
+            ts(w("GG", k, 16 * NCH, 8), w("MM"), w("KC", k, k + 1), A.is_lt)
+        ts(w("GG", 4, 16 * NCH, 8), w("MM"), 0.0, A.is_gt)
+        scan(w("XS"), w("GG"), w("CH", 1, 32 * NCH, 2))
+        new = "AL%d" % t
+        tt(w(new, 0, 28, 2), w("XS", 7, 224, 16), w("XS", 239, 448, 16), A.add)
+        tt(w(new, 1, 27, 2), w("XS", 247, 448, 16), w("XS", 15, 216, 16), A.add)
+        copy("v", w("LS%d" % t), w(new, 16, 28))
+        send(T["LR%d" % t][:], T["LS%d" % t][:], ("LS%d" % t, 0, 128, 0, 12, 1), "l%d" % t)
+        copy("v", w("LO%d" % t), w(new, 0, 16))
+
+    def layer(h, bs=range(4)):
+        z = (("ZOc", "ZOs"), ("ZRc", "ZRs"))[h]
+        m = (NO, NR)[h]
+        return [product([("Wc", "Ws", 128 * b), ("CTc", "CTs", 128 * b)], z, 0, m) for b in bs]
+
+    def state(h, outs, qs, bs=range(4)):
+        c0, c1 = PARTS[h]
+        for b in bs:
+            copy(qs[b], w("X", 4 * c0 + b, 4 * c1, 4), outs[b], 2.0 ** -6)
+
+    def addresses_out():
+        copy("v", w("OAF", 0, 14), w("AL%d" % (ROUNDS - 1), 0, 14))
+        copy("v", w("OAF", 14, 24), w("LR%d" % (ROUNDS - 1), 0, 10))
+        turn(w("OAT"), w("OAF"))
+        for k in range(8):
+            p0 = 32 * (k // 2)
+            dma("y", T.oa[k:k + 1, :], T.OAT[p0:p0 + 24, 16 * (k % 2):16 * (k % 2) + 16], [("OAT", p0, p0 + 24, 0, 32, 1)])
+
+    sa = score(0, 0)
+    sb = score(0, 1)
+    for t in range(ROUNDS):
+        last = t + 1 == ROUNDS
+        fa = unpack(("Qc%d" % t, "Qs%d" % t), "FO", 0, "ssss")
+        if t == 0:
+            bits(sa, 0)
+            edges(0)
+            bits(sb, 1)
+            edges(1)
+            for ph in range(4):
+                copy("sv"[ph % 2], w("D1", 2 * ph + 1, 768, 8), w("TAB", 192 * ph, 192 * ph + 96), w("SC"))
+                copy("vs"[ph % 2], w("D0", 2 * ph + 1, 768, 8), w("TAB", 192 * ph + 96, 192 * ph + 192), w("SC"))
+            choose(0)
+            turns(0, "EO", "CE", 32)
+        else:
+            bits(sb, 1)
+            edges(1)
+        choose(1)
+        gather("s", w("RO", 0, 240), w("TW", 8, 776), w("L2O", 0, 15))
+        gather("v", w("RR", 0, 176), w("TW", 8, 776), w("L2R", 0, 11))
+        turns(1, "ER", "CE", 32)
+        start()
+        turns(1, "RR", "CH", 128)
+        tt(view("MM", 0, 2 * NCH, 2, 0, 32), view("MA", 0, NCH, 1, 0, 32), view("MB", 0, NCH, 1, 0, 32), A.mult)
+        turns(0, "RO", "CH", 128)
+        take(fa)
+        take(unpack(("Qc%d" % t, "Qs%d" % t), "FO", 1, "ssss"))
+        carries(t)
+        take(unpack(("Ac%d" % t, "As%d" % t), "FP", 0, "ssss"))
+        for b in range(4):
+            gather("vsvs"[b], w("ZO", b, 4 * NO, 4), w("FO", C * b, C * b + C), w("LO%d" % t, 0, 14))
+        quant("ZOc", "ZOs", "ZO", 0, NO, 0)
+        take(unpack(("Ac%d" % t, "As%d" % t), "FP", 1, "vsvs"))
+        outs = layer(0)
+        if t == 0:
+            quant("Vc", "Vs", "VB", 0, 128, 0)
+        if not last:
+            ts(w("L2O", 0, 16), w("AL%d" % t, 0, 16), 2.0, A.mult)
+        for b in range(4):
+            gather("vsvs"[b], w("ZR", b, 4 * NR, 4), w("FP", C * b, C * b + C), w("LR%d" % t, 0, 10))
+        quant("ZRc", "ZRs", "ZR", 0, NR, 0)
+        outs2 = layer(1, (0, 1))
+        if last:
+            addresses_out()
+        state(0, outs, "svsv")
+        quant_x(t + 1, 0)
+        if not last:
+            send_x(t + 1, 0, NO, 0)
+            sa = score(t + 1, 0)
+            ts(w("L2R", 0, 12), w("LR%d" % t), 2.0, A.mult)
+        outs2 += layer(1, (2, 3))
+        if last:
+            state(1, outs2, "svsv")
+        else:
+            state(1, outs2, "svss", (0, 1))
+            bits(sa, 0)
+            edges(0)
+            choose(0)
+            state(1, outs2, "svss", (2, 3))
+            turns(0, "EO", "CE", 32)
+        quant_x(t + 1, 1)
+        if not last:
+            send_x(t + 1, NO, C, 1)
+            sb = score(t + 1, 1)
+
+    qc, qs = "Qc%d" % ROUNDS, "Qs%d" % ROUNDS
+    for h, (c0, c1) in enumerate(PARTS):
+        out = product([("Vc", "Vs", 0)], (qc, qs), c0, c1)
+        dma("ys"[h], T.oc[:, 4 * c0:4 * c1], T[qc][:, c0:c1].bitcast(dt.uint8), [(qc, 0, 128, c0, c1, 1)])
+        copy("sv"[h], w("Y", c0, c1), out)
+        dma("ys"[h], T.y[:, c0:c1], T.Y[:, c0:c1], [("Y", 0, 128, c0, c1, 1)])
+    for k in range(4):
+        dma("y", T.osc[4 * k:4 * k + 4, :], T[qs][32 * k:32 * k + 4, :], [(qs, 0, 128, 0, C, 1)])
+
+    for s in sorted(count):
+        if need_end.get(s, 0) < count[s]:
+            g.wait_ge(T.sem[s], count[s])

@@ -1,42 +1,39 @@
+import numpy as np
 from concourse.mybir import dt, AluOpType, ActivationFunctionType
 
 CODES = "float8_e4m3fn_x4"
 C, NO, NR, ROUNDS = 384, 224, 160, 3
 PARTS = ((0, NO), (NO, C))
-Q2 = (0, 4, 8, 12)
-EVEN0, ODD0 = 15, 3
-NCH = 28
-A_ROW = 9
-EDGE_ROWS = (4, 6)
+LC, LO = C // 16, NO // 16
+A0, B0 = 15, 3
+CLOSE = [2 ** (A0 + k) for k in range(4)]
+WIDE = [2 ** (B0 + 4 * k) for k in range(4)]
+WORD, DIFF, ADDR, EDGE = 4, 5, 9, 10
 
-_F = "float32"
+_F, _I, _B, _U = "float32", "int32", "bfloat16", "uint16"
 SCRATCH = {
-    "NX": ("sbuf", [128, 192], "int32"), "CI": ("sbuf", [128, 192], "int32"), "NI": ("sbuf", [128, 192], "int32"),
-    "NT": ("sbuf", [128, 192], "int32"), "ND": ("sbuf", [128, 192], _F), "AT": ("sbuf", [128, 48], _F), "NF": ("sbuf", [128, 192], _F),
-    "U4": ("sbuf", [128, 192], _F), "UU": ("sbuf", [128, 192], _F), "UT": ("sbuf", [128, 192], _F), "V2": ("sbuf", [128, 192], _F),
-    "V4": ("sbuf", [128, 192], _F), "SE": ("sbuf", [128, 192], _F), "SO": ("sbuf", [128, 192], _F), "FE": ("sbuf", [128, 192], _F),
-    "FD": ("sbuf", [128, 192], _F), "HE": ("sbuf", [128, 192], _F), "HO": ("sbuf", [128, 192], _F),
-    "ZZ": ("sbuf", [128, 16 * NCH], _F), "AW": ("sbuf", [128, C], _F), "M9": ("sbuf", [128, 1], _F), "SC": ("sbuf", [128, 1], _F),
-    "TAB": ("sbuf", [128, 768], _F), "D0": ("sbuf", [128, 768], _F), "D1": ("sbuf", [128, 768], _F),
-    "TW": ("sbuf", [128, 776], _F), "RO": ("sbuf", [128, 256], _F), "RR": ("sbuf", [128, 192], _F),
-    "EO": ("sbuf", [128, 256], "bfloat16"), "ER": ("sbuf", [128, 192], "bfloat16"),
-    "CH": ("sbuf", [128, 32 * NCH], _F), "CE": ("sbuf", [128, 32 * NCH], "bfloat16"),
-    "MA": ("sbuf", [128, NCH], _F), "MB": ("sbuf", [128, NCH], _F),
-    "MM": ("sbuf", [128, 2 * NCH], "int32"), "YY": ("sbuf", [128, NCH], "int32"),
-    "GG": ("sbuf", [128, 16 * NCH], _F), "XS": ("sbuf", [128, 16 * NCH], _F),
-    "PI": ("sbuf", [128, 1], "int32"), "P15": ("sbuf", [128, 1], "int32"), "PU": ("sbuf", [128, 1], "int32"),
-    "P31": ("sbuf", [128, 1], "int32"), "PUF": ("sbuf", [128, 1], _F), "PLF": ("sbuf", [128, 1], _F), "PHF": ("sbuf", [128, 1], _F),
-    "E3": ("sbuf", [128, 1], "int32"), "E4": ("sbuf", [128, 1], "int32"), "KC": ("sbuf", [128, 4], _F),
-    "LP": ("sbuf", [128, 8], "int32"), "LPU": ("sbuf", [128, 8], "uint16"),
-    "ALI": ("sbuf", [128, 24], "int32"), "OAF": ("sbuf", [128, 32], _F), "OAT": ("sbuf", [128, 32], _F),
-    "L2O": ("sbuf", [128, 16], "uint16"), "L2R": ("sbuf", [128, 16], "uint16"),
-    "CT": ("sbuf", [128, 2048], "bfloat16"), "CTc": ("sbuf", [128, 512], CODES), "CTs": ("sbuf", [128, 512], "uint8"),
-    "UB": ("sbuf", [128, 512], "bfloat16"), "Uc": ("sbuf", [128, 128], CODES), "Us": ("sbuf", [128, 128], "uint8"),
+    "NX": ("sbuf", [128, 192], _I), "NT": ("sbuf", [128, 12, 4, 4], _I), "CI": ("sbuf", [128, 192], _I), "NI": ("sbuf", [128, 12, 4, 4], _I),
+    "U4": ("sbuf", [128, 192], _F), "UA": ("sbuf", [128, 192], _F), "V2": ("sbuf", [128, 192], _F), "UB": ("sbuf", [128, 192], _F),
+    "SE": ("sbuf", [128, 192], _F), "SO": ("sbuf", [128, 192], _F), "HE": ("sbuf", [128, 192], _F), "HO": ("sbuf", [128, 192], _F),
+    "TT": ("sbuf", [128, 12, 4, 16], _F), "ZZ": ("sbuf", [128, C], _F),
+    "D0": ("sbuf", [128, 768], _F), "D1": ("sbuf", [128, 768], _F), "TW": ("sbuf", [128, 776], _F),
+    "RD": ("sbuf", [128, 2 * C], _F), "CH": ("sbuf", [128, LC, 32], _F),
+    "ED": ("sbuf", [128, LC, 2, 16], _B), "CE": ("sbuf", [128, LC, 32], _B),
+    "MI": ("sbuf", [128, LC], _I), "M1": ("sbuf", [128, LC], _I), "MS": ("sbuf", [128, LC], _I), "YY": ("sbuf", [128, 5, LC], _I),
+    "Y4": ("sbuf", [128, 4 * LC], _I), "Z4": ("sbuf", [128, 4 * LC], _I), "ZF": ("sbuf", [128, 4 * LC], _F), "PP": ("sbuf", [128, 4 * LC], _F),
+    "HM": ("sbuf", [128, 4 * LC], _F), "WS": ("sbuf", [128, LC], _F),
+    "GG": ("sbuf", [128, 5 * LC], _F), "NS": ("sbuf", [128, 5 * LC], _F), "XS": ("sbuf", [128, 5 * LC], _F),
+    "PI": ("sbuf", [128, 1], _I), "P15": ("sbuf", [128, 1], _I), "PUI": ("sbuf", [128, 1], _I), "PU": ("sbuf", [128, 1], _F),
+    "IDL": ("sbuf", [128, 1], _F), "SCP": ("sbuf", [128, 1], _F), "KC": ("sbuf", [128, 4], _F), "EE": ("sbuf", [128, 2], _F),
+    "LP": ("sbuf", [128, 8], _I), "LPU": ("sbuf", [128, 8], _U),
+    "ALI": ("sbuf", [128, LC], _I), "L2": ("sbuf", [128, 2 * LC], _U), "OAF": ("sbuf", [128, 32], _F), "OAT": ("sbuf", [128, 32], _F),
+    "CT": ("sbuf", [128, 516], _B), "CTc": ("sbuf", [128, 512], CODES), "CTs": ("sbuf", [128, 512], "uint8"),
+    "UU": ("sbuf", [128, 512], _B), "Uc": ("sbuf", [128, 128], CODES), "Us": ("sbuf", [128, 128], "uint8"),
     "Pc": ("sbuf", [128, 128], CODES), "Ps": ("sbuf", [128, 128], "uint8"),
-    "VB": ("sbuf", [128, 512], "bfloat16"), "Vc": ("sbuf", [128, 128], CODES), "Vs": ("sbuf", [128, 128], "uint8"),
+    "VB": ("sbuf", [128, 512], _B), "Vc": ("sbuf", [128, 128], CODES), "Vs": ("sbuf", [128, 128], "uint8"),
     "Wc": ("sbuf", [128, 512], CODES), "Ws": ("sbuf", [128, 512], "uint8"),
-    "X": ("sbuf", [128, 4 * C], "bfloat16"), "FO": ("sbuf", [128, 4 * C], "bfloat16"), "FP": ("sbuf", [128, 4 * C], "bfloat16"),
-    "ZO": ("sbuf", [128, 4 * NO], "bfloat16"), "ZR": ("sbuf", [128, 4 * NR], "bfloat16"),
+    "X": ("sbuf", [128, 4 * C], _B), "FO": ("sbuf", [128, 8 * C], _B), "FP": ("sbuf", [128, 8 * C], _B),
+    "ZO": ("sbuf", [128, 4 * NO], _B), "ZR": ("sbuf", [128, 4 * NR], _B),
     "ZOc": ("sbuf", [128, NO], CODES), "ZOs": ("sbuf", [128, NO], "uint8"),
     "ZRc": ("sbuf", [128, NR], CODES), "ZRs": ("sbuf", [128, NR], "uint8"),
     "Y": ("sbuf", [128, C], _F),
@@ -45,15 +42,16 @@ for _t in range(ROUNDS + 1):
     SCRATCH["Qc%d" % _t] = ("sbuf", [128, C], CODES)
     SCRATCH["Qs%d" % _t] = ("sbuf", [128, C], "uint8")
 for _t in range(ROUNDS):
-    SCRATCH["AL%d" % _t] = ("sbuf", [128, NCH], _F)
     SCRATCH["Ac%d" % _t] = ("sbuf", [128, C], CODES)
     SCRATCH["As%d" % _t] = ("sbuf", [128, C], "uint8")
-    SCRATCH["LO%d" % _t] = ("sbuf", [128, 16], "uint16")
-    SCRATCH["LS%d" % _t] = ("sbuf", [128, 12], "uint16")
-    SCRATCH["LR%d" % _t] = ("sbuf", [128, 12], "uint16")
+    SCRATCH["LA%d" % _t] = ("sbuf", [128, LC], _U)
+    SCRATCH["LR%d" % _t] = ("sbuf", [128, LC - LO], _U)
 for _t in range(8):
     SCRATCH["pb%d" % _t] = ("psum", [128, 512], _F)
-SEMAPHORES = ["cv", "cs", "ct", "cg", "sent"] + ["d%d" % i for i in range(48)] + ["q%d%d" % (t, h) for t in range(ROUNDS) for h in range(2)] + ["l%d" % t for t in range(ROUNDS)]
+SEMAPHORES = ["cv", "cs", "ct", "cg", "sent"] + ["d%d" % i for i in range(32)] + ["q%d%d" % (t, h) for t in range(ROUNDS) for h in range(2)] + ["l%d" % t for t in range(ROUNDS)]
+PICKS = (("v", 0, 8), ("s", 8, 16), ("s", 16, 24))
+S = slice
+ALL = slice(None)
 
 
 def rank_program(g, core, T, topo):
@@ -67,54 +65,49 @@ def rank_program(g, core, T, topo):
     A = AluOpType
     ACT = ActivationFunctionType
     queue = {"v": g.vector, "s": g.scalar, "t": g.tensor, "g": g, "y": g.sync}
-    count, seen, hist, need_end = {}, {}, {}, {}
+    count, hist, waited = {}, {}, {}
+    known = {q: {} for q in queue}
+    behind = {}
 
-    def view(name, c0, c1, step=1, p0=0, p1=128):
-        buf = T[name]
-        if step != 1:
-            ap = buf[p0:p1, c0:c1:step]
-        elif (p0, p1) == (0, 128):
-            ap = buf[:, c0:c1]
-        else:
-            ap = buf[p0:p1, c0:c1]
-        return (ap, (name, p0, p1, c0, c1, step))
+    def v(name, *idx, p=(0, 128)):
+        shape = T[name].shape
+        idx = idx + (ALL,) * (len(shape) - 1 - len(idx))
+        hit = np.zeros(shape[1:], bool)
+        hit[idx] = True
+        bits = int.from_bytes(np.packbits(hit.reshape(-1)).tobytes(), "big")
+        return (T[name][(S(p[0], p[1]),) + idx], (name, p[0], p[1], bits))
 
-    def w(name, a=0, b=None, step=1):
-        return view(name, a, T[name].shape[1] if b is None else b, step)
-
-    def meet(a, b):
-        if a[1] >= b[2] or b[1] >= a[2] or a[3] >= b[4] or b[3] >= a[4]:
-            return False
-        return not (a[5] == b[5] and a[5] > 1 and (a[3] - b[3]) % a[5])
+    def w(name, a=0, b=None, step=1, p=(0, 128)):
+        return v(name, S(a, T[name].shape[1] if b is None else b, step), p=p)
 
     def waits(q, reads, writes):
         need = {}
-        for kind, rects in (("r", reads), ("w", writes)):
-            for r in rects:
+        for kind, places in (("r", reads), ("w", writes)):
+            for r in places:
                 bank = r[0].startswith("pb")
                 for hk, hq, hsem, hval, hr in hist.get(r[0], []):
                     if kind == "r" and hk == "r" and not (bank and hq != q):
                         continue
-                    if kind == "w" and hq == q and q in "vstg" and not hsem.startswith("d") and (hk == "r" or q == "t"):
+                    if bank and hq == q == "t":
                         continue
-                    if bank or meet(r, hr):
+                    if bank or (r[1] < hr[2] and hr[1] < r[2] and r[3] & hr[3]):
                         need[hsem] = max(need.get(hsem, 0), hval)
-        for s in sorted(need):
-            if seen.get((q, s), 0) < need[s]:
+        for s in sorted(need, key=lambda s: s == "c" + q):
+            if known[q].get(s, 0) < need[s]:
                 queue[q].wait_ge(T.sem[s], need[s])
-                seen[(q, s)] = need[s]
-                need_end[s] = max(need_end.get(s, 0), need[s])
+                waited[s] = max(waited.get(s, 0), need[s])
+                known[q][s] = need[s]
+                for s2, k in behind.get((s, need[s]), {}).items():
+                    known[q][s2] = max(known[q].get(s2, 0), k)
 
     def note(q, sem, val, reads, writes):
-        for kind, rects in (("r", reads), ("w", writes)):
-            for r in rects:
-                lst = hist.setdefault(r[0], [])
-                if kind == "w" and r[5] == 1:
-                    lst[:] = [h for h in lst if not (h[4][1] >= r[1] and h[4][2] <= r[2] and h[4][3] >= r[3] and h[4][4] <= r[4] and h[1] == q)]
-                lst.append((kind, q, sem, val, r))
+        behind[(sem, val)] = dict(known[q])
+        for kind, places in (("r", reads), ("w", writes)):
+            for r in places:
+                hist.setdefault(r[0], []).append((kind, q, sem, val, r))
 
     def op(q, call, reads, writes):
-        reads = [a[1] for a in reads]
+        reads = [a[1] for a in reads if isinstance(a, tuple)]
         writes = [a[1] for a in writes]
         waits(q, reads, writes)
         sem = "c" + q
@@ -125,7 +118,7 @@ def rank_program(g, core, T, topo):
     n_dma = [0]
 
     def dma(q, out, in_, reads=(), writes=()):
-        reads, writes = list(reads), list(writes)
+        reads, writes = [a[1] for a in reads], [a[1] for a in writes]
         waits(q, reads, writes)
         sem = "d%d" % n_dma[0]
         n_dma[0] += 1
@@ -133,25 +126,32 @@ def rank_program(g, core, T, topo):
         queue[q].dma_start(out, in_).then_inc(T.sem[sem], 16)
         note(q, sem, 16, reads, writes)
 
-    def load(q, name, src, c0=0, c1=None):
-        v = w(name, c0, c1)
-        dma(q, v[0].bitcast(dt.uint8) if name == "Wc" else v[0], src, (), [v[1]])
+    def load(q, name, src, c0=0, c1=None, after=()):
+        d = w(name, c0, c1)
+        dma(q, d[0].bitcast(dt.uint8) if name == "Wc" else d[0], src, after, [d])
 
-    def lands(name, c0, c1, sem, val):
-        hist.setdefault(name, []).append(("w", "far", sem, val, (name, 0, 128, c0, c1, 1)))
+    def lands(place, sem, val):
+        hist.setdefault(place[1][0], []).append(("w", "far", sem, val, place[1]))
         count[sem] = max(count.get(sem, 0), val)
 
-    def send(out, in_, rect, sem):
-        waits("g", [rect], [])
+    def send(out, in_, sem, codes=False):
+        waits("g", [in_[1]], [])
         count["sent"] = count.get("sent", 0) + len(topo.engines(core, nxt))
-        g.remote_dma(out, in_, T.sem[sem], T.sem.sent, pid, rid, topo.mask(core, nxt))
+        a, b = (out[0].bitcast(dt.uint8), in_[0].bitcast(dt.uint8)) if codes else (out[0], in_[0])
+        g.remote_dma(a, b, T.sem[sem], T.sem.sent, pid, rid, topo.mask(core, nxt))
 
-    def fill(ap, val):
-        op("v", lambda e: e.memset(ap[0], val), [], [ap])
+    def ap(a):
+        return a[0] if isinstance(a, tuple) else a
+
+    def fill(out, val):
+        op("v", lambda e: e.memset(out[0], val), [], [out])
 
     def act(out, in_, func=ACT.Copy, scale=1.0, bias=0.0):
-        a = scale[0] if isinstance(scale, tuple) else scale
-        op("s", lambda e: e.activation(out[0], in_[0], func, bias=bias, scale=a), [in_] + ([scale] if isinstance(scale, tuple) else []), [out])
+        op("s", lambda e: e.activation(out[0], in_[0], func, bias=ap(bias), scale=ap(scale)), [in_, scale, bias], [out])
+
+    def const(out, val):
+        k = int(np.prod(out[0].shape[1:]))
+        act(out, w("ZZ", 0, k, p=out[1][1:3]), ACT.Identity if val else ACT.Copy, 1.0, float(val))
 
     def copy(q, out, in_, scale=None):
         if q == "s":
@@ -162,13 +162,10 @@ def rank_program(g, core, T, topo):
             ts(out, in_, scale, A.mult)
 
     def ts(out, in_, s1, o1, s2=None, o2=None):
-        reads = [in_] + [s for s in (s1, s2) if isinstance(s, tuple)]
-        a1 = s1[0] if isinstance(s1, tuple) else s1
-        a2 = s2[0] if isinstance(s2, tuple) else s2
         if o2 is None:
-            op("v", lambda e: e.tensor_scalar(out[0], in_[0], a1, None, o1), reads, [out])
+            op("v", lambda e: e.tensor_scalar(out[0], in_[0], ap(s1), None, o1), [in_, s1], [out])
         else:
-            op("v", lambda e: e.tensor_scalar(out[0], in_[0], a1, a2, o1, o2), reads, [out])
+            op("v", lambda e: e.tensor_scalar(out[0], in_[0], ap(s1), ap(s2), o1, o2), [in_, s1, s2], [out])
 
     def tt(out, a, b, o):
         op("v", lambda e: e.tensor_tensor(out[0], a[0], b[0], o), [a, b], [out])
@@ -187,195 +184,206 @@ def rank_program(g, core, T, topo):
             op(q, lambda e: e.tensor_copy(out[0], src), [win, off], [out])
 
     def quant(c, s, tile, c0, c1, t0):
-        qc, qs, x = view(c, c0, c1), view(s, c0, c1), view(tile, t0, t0 + 4 * (c1 - c0))
+        qc, qs, x = w(c, c0, c1), w(s, c0, c1), w(tile, t0, t0 + 4 * (c1 - c0))
         op("v", lambda e: e.quantize_mx(qc[0], qs[0], x[0]), [x], [qc, qs])
 
-    bank = [0]
-
-    def product(pairs, rhs, c0, c1):
-        out = view("pb%d" % (bank[0] % 8), 0, c1 - c0)
-        bank[0] += 1
-        rc, rs = view(rhs[0], c0, c1), view(rhs[1], c0, c1)
+    def product(bank, pairs, rhs, c0, c1):
+        out = w("pb%d" % bank, 0, c1 - c0)
+        rc, rs = w(rhs[0], c0, c1), w(rhs[1], c0, c1)
         for i, (c, s, a) in enumerate(pairs):
-            lc, ls = view(c, a, a + 128), view(s, a, a + 128)
+            lc, ls = w(c, a, a + 128), w(s, a, a + 128)
             first, last = i == 0, i == len(pairs) - 1
             op("t", lambda e: e.matmul_mx(out[0], lc[0], ls[0], rc[0], rs[0], first, last), [lc, ls, rc, rs], [out])
         return out
-
-    for t in range(ROUNDS):
-        for h, (c0, c1) in enumerate(PARTS):
-            for name in ("Ac%d" % t, "As%d" % t):
-                lands(name, c0, c1, "q%d%d" % (t, h if t else 0), 2 * n_in)
-        lands("LR%d" % t, 0, 12, "l%d" % t, n_in)
-
-    load("y", "NX", T.nx[:])
-    load("s", "X", T.x[:, 0:4 * NO], 0, 4 * NO)
-    load("y", "X", T.x[:, 4 * NO:4 * C], 4 * NO, 4 * C)
-    load("s", "UB", T.u[:])
-    load("y", "ALI", T.al[:])
-    load("y", "Wc", T.wc[:])
-    load("s", "Ws", T.ws[:])
-    load("y", "VB", T.v[:])
 
     def iota(out, pattern, base, mult, loose=False):
         if loose:
             op("g", lambda e: e.iota(out[0], pattern, base, mult, allow_small_or_imprecise_dtypes=True), [], [out])
         else:
             op("g", lambda e: e.iota(out[0], pattern, base, mult), [], [out])
-    iota(w("PI"), [[1, 1]], 0, 1)
-    for b in range(2):
-        iota(w("AT", 24 * b, 24 * b + 24), [[128, 3], [0, 2], [1, 4]], 0, 0, True)
-    iota(w("LP"), [[16, 8]], 0, 0)
-    iota(w("AW"), [[1, C]], 0, 0, True)
-    iota(w("CT"), [[0, 2048]], 0, 0, True)
-    for b in range(4):
-        d = view("CT", 512 * b + b, 512 * b + 512, 4)
-        op("g", lambda e: e.affine_select(d[0], d[0], [[-1, 128]], A.not_equal, 64.0, 0, 1), [d], [d])
-    fill(w("ZZ"), 0.0)
-    ts(w("P15"), w("PI"), 15, A.bitwise_and)
-    ts(w("P31"), w("PI"), 31, A.bitwise_and)
-    ts(w("M9"), w("P15"), A_ROW, A.is_equal)
-    ts(w("PHF"), w("P31"), 4.0, A.mult)
-    for ph in range(4):
-        act(w("TAB", 192 * ph, 192 * ph + 96), w("AW", ph, C, 4), ACT.Copy, w("M9"))
-        copy("s", w("TAB", 192 * ph + 96, 192 * ph + 192), w("ZZ", 0, 96))
-    copy("s", w("D0", 0, 768, 2), w("ZZ", 0, 384))
-    for name in ("RO", "RR", "EO", "ER", "OAF"):
-        copy("s", w(name), w("ZZ", 0, T[name].shape[1]))
-    ts(w("AT"), w("AT"), w("PHF"), A.add)
-    for name, ratio in (("HE", 2.0), ("HO", 16.0)):
-        fill(w(name), ratio)
-        fill(w(name, 0, 192, 4), 0.0)
-    ts(w("SC"), w("P15"), 0, A.is_equal, 2.0 ** (ODD0 - EVEN0 - 3) - 1.0, A.mult)
-    ts(w("PU"), w("PI"), 4, A.logical_shift_right, 1, A.bitwise_and)
-    ts(w("E3"), w("P15"), EDGE_ROWS[0], A.is_equal)
-    ts(w("E4"), w("P15"), EDGE_ROWS[1], A.is_equal, 17, A.mult)
-    ts(w("SC"), w("SC"), 1.0, A.add)
-    copy("v", w("PUF"), w("PU"))
-    tt(w("LP", 0, 1), w("E3"), w("E4"), A.add)
-    ts(w("PLF"), w("PUF"), -1.0, A.mult, 1.0, A.add)
-    copy("v", w("LPU"), w("LP"))
-    for k in range(1, 4):
-        lo, up = 2.0 ** (EVEN0 + k), 2.0 ** (ODD0 + Q2[k])
-        ts(w("KC", k, k + 1), w("PUF"), up - lo, A.mult, lo, A.add)
 
-    ts(w("CI"), w("NX"), 9, A.logical_shift_right)
-    ts(w("U4"), w("CI"), 4.0, A.mult, -8.0, A.add)
-    tt(w("UU"), w("CI"), w("U4"), A.max)
-    turn(w("UT"), w("UU"))
-    act(w("V2"), w("UT"), ACT.Square)
-    act(w("V4"), w("V2"), ACT.Square)
-    scan(w("SO"), w("HO"), w("UT"))
-    ts(w("NI"), w("NX"), 511, A.bitwise_and)
-    turn(w("FD"), w("SO"))
-    turn(w("NT"), w("NI"))
-    scan(w("SE"), w("HE"), w("V4"))
-    tt(w("FD", 96, 192), w("FD", 96, 192), w("FD", 0, 96), A.subtract)
-    turn(w("FE"), w("SE"))
-    for e in range(3):
-        tt(w("ND", e, 192, 4), w("NT", e, 192, 4), w("NT", e + 1, 192, 4), A.subtract)
-    tt(w("ND", 3, 192, 4), w("NT", 3, 192, 4), w("AT"), A.subtract)
-    tt(w("FE", 96, 192), w("FE", 96, 192), w("FE", 0, 96), A.subtract)
-    turn(w("NF"), w("ND"))
-    tt(w("NF", 96, 192), w("NF", 96, 192), w("NF", 0, 96), A.subtract)
+    def mark(d, pattern, val, base):
+        op("g", lambda e: e.affine_select(d[0], d[0], pattern, A.not_equal, val, base, 1), [d], [d])
 
-    def to_row(q, name, e, r):
-        dma(q, T.TAB[r:128:16, :], T[name][e:128:4, :], [(name, 0, 128, 0, 192, 1), ("TAB", 16, 128, 0, 768, 1)], [("TAB", r, r + 1, 0, 768, 1)])
-    to_row("s", "FD", 3, 2)
-    to_row("y", "FE", 3, 0)
-    for e in range(4):
-        to_row("sysy"[e], "NF", e, 1 + 2 * e)
-    act(w("GG"), w("ZZ"), ACT.Identity, 1.0, 1.0)
-    copy("s", w("GG", 0, 16 * NCH, 8), w("ZZ", 0, 2 * NCH))
     for t in range(ROUNDS):
-        copy("s", w("AL%d" % t, 27, 28), w("ZZ", 0, 1))
+        for h, (c0, c1) in enumerate(PARTS):
+            for name in ("Ac%d" % t, "As%d" % t):
+                lands(w(name, c0, c1), "q%d%d" % (t, h if t else 0), 2 * n_in)
+        lands(w("LR%d" % t), "l%d" % t, n_in)
+    Q = [(32 * k, 32 * k + 32) for k in range(4)]
+
+    load("y", "NX", T.nx[:])
+    load("s", "UU", T.u[:])
+    load("y", "X", T.x[:, 0:4 * NO], 0, 4 * NO)
+    load("y", "X", T.x[:, 4 * NO:4 * C], 4 * NO, 4 * C)
+    load("y", "ALI", T.al[:])
+    load("y", "Wc", T.wc[:], after=[w("X")])
+    load("y", "Ws", T.ws[:])
+    load("y", "VB", T.v[:])
+
+    fill(w("CT"), 0.0)
+    fill(w("ZZ"), 0.0)
+    fill(w("EE"), 1.0)
+    iota(w("PI"), [[1, 1]], 0, 1)
+    mark(w("CT", 3, 515, 4), [[-1, 128]], 64.0, 0)
+    iota(w("LP"), [[16, 8]], 0, 0)
+    iota(v("TT", S(0, 6), ALL, ADDR), [[128, 3], [0, 2], [1, 4]], 0, 4, True)
+    mark(w("EE", 0, 1), [[0, 1]], 3.0 * CLOSE[0], -EDGE)
+    mark(w("EE", 1, 2), [[0, 1]], 1.0 * CLOSE[0], -EDGE)
+    const(w("HO"), 16)
+    const(w("HE"), 2)
+    const(v("TT", ALL, ALL, S(EDGE, 16)), 0)
+    const(v("TT", ALL, ALL, S(0, 4)), 0)
+    const(w("HO", 0, 192, 4), 0)
+    const(w("HE", 0, 192, 4), 0)
+    const(v("TT", S(6, 12), ALL, ADDR), 0)
+    for k in range(1, 4):
+        a = v("TT", S(0, 6), ALL, ADDR, p=Q[k])
+        act(a, a, ACT.Identity, 1.0, -128.0 * k)
+    const(w("D0", 0, 768, 2), 0)
+    ts(w("P15"), w("PI"), 15, A.bitwise_and)
+    ts(w("PUI"), w("PI"), 4, A.logical_shift_right, 1, A.bitwise_and)
+    for b in range(4):
+        quant("CTc", "CTs", "CT", 128 * b, 128 * b + 128, 3 - b)
+    ts(w("LPU", 0, 1), w("P15"), 16.0, A.mult, 1.0 - 16.0 * EDGE, A.add)
+    copy("v", w("LPU", 1, 8), w("LP", 1, 8))
+    copy("v", w("PU"), w("PUI"))
+    same = (sum(WIDE[k] / CLOSE[k] for k in range(4)), sum(CLOSE[k] / WIDE[k] for k in range(4)))
+    for p, word in (((0, 64), same[0]), (Q[2], same[1]), (Q[3], same[0])):
+        ts(w("IDL", p=p), w("PUI", p=p), -word, A.mult, word, A.add)
+    fill(w("Z4"), 0)
+    fill(w("OAF"), 0.0)
 
     def send_x(t, c0, c1, h):
-        for a, b in (("Qc%d", "Ac%d"), ("Qs%d", "As%d")):
-            s, d = T[a % t][:, c0:c1], T[b % t][:, c0:c1]
-            if a == "Qc%d":
-                s, d = s.bitcast(dt.uint8), d.bitcast(dt.uint8)
-            send(d, s, (a % t, 0, 128, c0, c1, 1), "q%d%d" % (t, h))
+        send(w("Ac%d" % t, c0, c1), w("Qc%d" % t, c0, c1), "q%d%d" % (t, h), True)
+        send(w("As%d" % t, c0, c1), w("Qs%d" % t, c0, c1), "q%d%d" % (t, h))
 
     def quant_x(t, h):
         c0, c1 = PARTS[h]
         quant("Qc%d" % t, "Qs%d" % t, "X", c0, c1, 4 * c0)
 
-    quant_x(0, 0)
-    quant_x(0, 1)
-    send_x(0, 0, C, 0)
-    quant("Uc", "Us", "UB", 0, 128, 0)
-    op("v", lambda e: e.tensor_copy(T.Pc[:, 0:128].bitcast(dt.uint32), T.Uc[:, 0:128].bitcast(dt.uint32).indirect(T.LPU[:, 0:8])), [w("Uc"), w("LPU")], [w("Pc")])
-    op("v", lambda e: e.tensor_copy(T.Ps[:, 0:128], T.Us[:, 0:128].indirect(T.LPU[:, 0:8])), [w("Us"), w("LPU")], [w("Ps")])
-    for name, o, a, b in (("L2O", 0, 0, 14), ("L2O", 14, 0, 2), ("L2R", 0, 14, 24), ("L2R", 10, 14, 16)):
-        ts(w(name, o, o + b - a), w("ALI", a, b), 2.0, A.mult)
-    ts(w("GG", 5, 16 * NCH, 16), w("ZZ", 0, NCH), w("PLF"), A.add)
-    ts(w("GG", 13, 16 * NCH, 16), w("ZZ", 0, NCH), w("PUF"), A.add)
-    quant("CTc", "CTs", "CT", 0, 512, 0)
-
     def score(t, h):
         c0, c1 = PARTS[h]
-        return product([("Pc", "Ps", 0)], ("Qc%d" % t, "Qs%d" % t), c0, c1)
-
-    def unpack(src, dst, h, qs):
-        c0, c1 = PARTS[h]
-        outs = [product([("CTc", "CTs", 128 * b)], src, c0, c1) for b in range(4)]
-        return [(qs[b], w(dst, C * b + c0, C * b + c1), outs[b]) for b in range(4)]
-
-    def take(jobs):
-        for q, out, ps in jobs:
-            copy(q, out, ps, 2.0 ** -6)
+        return product(h, [("Pc", "Ps", 0)], ("Qc%d" % t, "Qs%d" % t), c0, c1)
 
     def bits(ps, h):
         c0, c1 = PARTS[h]
         ts(w("D1", 2 * c0, 2 * c1, 2), ps, 0.0, A.is_gt)
 
-    def choose(h):
-        c0, c1 = PARTS[h]
-        scan(w("TW", 7 + 2 * c0, 7 + 2 * c1), w("D0", 2 * c0, 2 * c1), w("D1", 2 * c0, 2 * c1))
-
     def edges(h):
         c0, c1 = PARTS[h]
-        m, name = c1 - c0, ("EO", "ER")[h]
-        for a, b, o in ((0, m, 0), (0, 16, m)):
-            copy("s", view(name, o, o + b - a, 1, 0, 32), view("D1", 2 * (c0 + a), 2 * (c0 + b), 2, 0, 32))
+        for half in range(2):
+            act(v("ED", S(c0 // 16, c1 // 16), half, p=Q[0]), w("D1", 2 * c0, 2 * c1, 2, p=Q[0]), ACT.Identity, w("EE", 0, 1, p=Q[0]), w("EE", 1, 2, p=Q[0]))
 
-    def turns(h, src, dst, p1):
-        m = (14, 10)[h]
-        first, second = ((0, 14), (8, 22))[h]
-        turn(view(dst, 32 * first, 32 * first + 16 * (m + 2), 1, 0, p1), view(src, 0, 16 * (m + 2), 1, 0, p1))
-        turn(view(dst, 32 * second, 32 * second + 32, 1, 0, p1), view(src, 16 * (m - 1), 16 * (m + 1), 1, 0, p1))
-        turn(view(dst, 32 * second + 32, 32 * second + 32 + 16 * m, 1, 0, p1), view(src, 16, 16 * (m + 1), 1, 0, p1))
+    def turn_edges(h):
+        c = S(PARTS[h][0] // 16, PARTS[h][1] // 16)
+        turn(v("CE", c, p=Q[0]), v("ED", c, p=Q[0]))
 
-    def start():
-        p = lambda name, a, b, step: view(name, a, b, step, 0, 32)
-        act(p("MA", 0, NCH, 1), p("CE", EDGE_ROWS[0], 32 * NCH, 32), ACT.Identity, 3.0 * 2.0 ** EVEN0, 2.0 ** EVEN0)
-        act(p("MB", 0, NCH, 1), p("CE", EDGE_ROWS[1], 32 * NCH, 32), ACT.Identity, 1.0, 1.0)
+    def choose(c0, c1):
+        scan(w("TW", 7 + 2 * c0, 7 + 2 * c1), w("D0", 2 * c0, 2 * c1), w("D1", 2 * c0, 2 * c1))
 
-    def carries(t):
-        n2 = 2 * NCH
-        p = lambda name, a, b, step, q: view(name, a, b, step, 32 * q, 32 * q + 32)
-        masks = (sum(2 ** (ODD0 + k) for k in Q2), sum(2 ** (EVEN0 + k) for k in range(4)))
-        for s in range(7):
-            q, o = s // 2, s % 2
-            q2, o2 = (s + 1) // 2, (s + 1) % 2
-            tt(p("YY", 0, NCH, 1, q), p("CH", (0, 18)[o], 32 * NCH, 32, q), p("MM", o, n2, 2, q), A.mult)
-            ts(p("MM", o2, n2, 2, q2), p("YY", 0, NCH, 1, q), masks[o], A.bitwise_and)
+    turn(v("NT"), w("NX"))
+    quant("Uc", "Us", "UU", 0, 128, 0)
+    ts(w("CI"), v("NT"), 9, A.logical_shift_right)
+    ts(v("NI"), v("NT"), 511, A.bitwise_and)
+    ts(w("U4"), w("CI"), 4.0, A.mult, -8.0, A.add)
+    op("v", lambda e: e.tensor_copy(T.Pc[:, 0:128].bitcast(dt.uint32), T.Uc[:, 0:128].bitcast(dt.uint32).indirect(T.LPU[:, 0:8])), [w("Uc"), w("LPU")], [w("Pc")])
+    gather("s", w("Ps"), w("Us"), w("LPU"))
+    tt(w("UA"), w("CI"), w("U4"), A.max)
+    act(w("V2"), w("UA"), ACT.Square)
+    act(w("UB"), w("V2"), ACT.Square)
+    tt(v("TT", ALL, ALL, S(DIFF, DIFF + 3)), v("NI", ALL, ALL, S(0, 3)), v("NI", ALL, ALL, S(1, 4)), A.subtract)
+    scan(w("SO"), w("HO"), w("UA"))
+    for b in range(2):
+        tt(v("TT", S(6 * b, 6 * b + 6), ALL, DIFF + 3), v("NI", S(6 * b, 6 * b + 6), ALL, 3), v("TT", S(0, 6), ALL, ADDR), A.subtract)
+    scan(w("SE"), w("HE"), w("UB"))
+    copy("s", v("TT", ALL, ALL, S(0, 4), p=Q[1]), w("UA", p=Q[1]), float(CLOSE[0]))
+    for k in (0, 2):
+        copy("s", v("TT", ALL, ALL, WORD, p=Q[k]), w("SO", 3, 192, 4, p=Q[k]), CLOSE[0] / WIDE[3])
+    copy("s", v("TT", ALL, ALL, S(0, 4), p=Q[2]), w("UB", p=Q[2]), float(WIDE[0]))
+    quant_x(0, 0)
+    sa = score(0, 0)
+    for k in (1, 3):
+        copy("s", v("TT", ALL, ALL, WORD, p=Q[k]), w("SE", 3, 192, 4, p=Q[k]), WIDE[0] / CLOSE[3])
+    for ph in range(4):
+        copy("sv"[ph % 2], v("TT", S(0, 12, 2), ph, WORD, p=Q[0]), w("SE", 4 * ph + 3, 192, 32, p=Q[0]), WIDE[0] / CLOSE[3])
+    quant_x(0, 1)
+    sb = score(0, 1)
+    send_x(0, 0, C, 0)
+    bits(sa, 0)
+    tt(v("TT", S(6, 12), ALL, S(0, ADDR)), v("TT", S(6, 12), ALL, S(0, ADDR)), v("TT", S(0, 6), ALL, S(0, ADDR)), A.subtract)
+    edges(0)
+    for ph in range(4):
+        turn(w("D1", 2 * ph + 1, 768, 8), v("TT", S(0, 6), ph))
+    bits(sb, 1)
+    edges(1)
+    for ph in range(4):
+        turn(w("D0", 2 * ph + 1, 768, 8), v("TT", S(6, 12), ph))
+    for half in range(2):
+        ts(w("L2", half, 2 * LC, 2), w("ALI"), 2.0, A.mult)
+    choose(0, C)
+    turn_edges(0)
+    const(w("HM"), 2)
+    const(w("GG", 0, 5 * LC, 5), 0)
+    const(w("SCP"), 1.0 / CLOSE[3])
+    for k in range(1, 4):
+        const(w("KC", k, k + 1), WIDE[k])
+    const(w("HM", p=Q[2]), 16)
+    const(w("SCP", p=Q[2]), 1.0 / WIDE[3])
+    for k in range(1, 4):
+        const(w("KC", k, k + 1, p=Q[2]), CLOSE[k])
+    const(w("HM", 0, 4 * LC, 4), 0)
+
+    def unpack(src, dst, banks, qs):
+        outs = [product(banks[b], [("CTc", "CTs", 128 * b)], src, 0, C) for b in range(4)]
+        return [(qs[b], w(dst, 2 * C * b, 2 * C * (b + 1), 2), outs[b]) for b in range(4)]
+
+    def take(jobs):
+        for q, out, ps in jobs:
+            copy(q, out, ps, 2.0 ** -6)
+
+    def carries(t, gaps):
+        close, wide = sum(CLOSE), sum(WIDE)
+        y = lambda i, p: v("YY", i, p=p)
+        for e in range(4):
+            tt(w("Y4", e, 4 * LC, 4, p=(0, 96)), v("CH", ALL, e, p=(0, 96)), v("CH", ALL, 16 + WORD, p=(0, 96)), A.mult)
+        act(w("WS"), v("CH", ALL, WORD), ACT.Identity, w("PU"), w("IDL"))
+        tt(y(0, Q[0]), v("CH", ALL, WORD, p=Q[0]), w("MI", p=Q[0]), A.mult)
+        ts(w("Z4", p=Q[1]), w("Y4", p=Q[1]), wide, A.bitwise_and)
+        ts(w("Z4", p=Q[2]), w("Y4", p=Q[2]), close, A.bitwise_and)
+        ts(w("M1", p=Q[0]), y(0, Q[0]), wide, A.bitwise_and)
+        ts(w("ZF", p=(0, 96)), w("Z4", p=(0, 96)), w("SCP", p=(0, 96)), A.mult)
+        tt(y(1, Q[0]), v("CH", ALL, 16 + WORD, p=Q[0]), w("M1", p=Q[0]), A.mult)
+        scan(w("PP", p=(0, 96)), w("HM", p=(0, 96)), w("ZF", p=(0, 96)))
+        ts(w("MI", p=Q[1]), y(1, Q[0]), close, A.bitwise_and)
+        copy("s", w("NS"), v("CH", ALL, S(16 + DIFF, 16 + ADDR + 1)))
+        take(gaps[:1])
+        for k in range(4):
+            p = (32 * k, 32 * k + 16)
+            copy("s", w("NS", p=p), v("CH", ALL, S(DIFF, ADDR + 1), p=p))
+        take(gaps[1:])
+        tt(y(2, Q[1]), w("PP", 3, 4 * LC, 4, p=Q[1]), w("MI", p=Q[1]), A.mult)
+        ts(w("MI", p=Q[2]), y(2, Q[1]), wide, A.bitwise_and)
+        tt(y(3, Q[2]), w("PP", 3, 4 * LC, 4, p=Q[2]), w("MI", p=Q[2]), A.mult)
+        tt(y(4, (0, 96)), w("WS", p=(0, 96)), w("MI", p=(0, 96)), A.mult)
+        ts(w("MI", p=Q[3]), y(3, Q[2]), close, A.bitwise_and)
+        ts(w("MS", p=(0, 64)), y(4, (0, 64)), wide, A.bitwise_and)
+        tt(y(4, Q[3]), w("WS", p=Q[3]), w("MI", p=Q[3]), A.mult)
+        ts(w("MS", p=Q[2]), y(4, Q[2]), close, A.bitwise_and)
+        ts(w("MS", p=Q[3]), y(4, Q[3]), wide, A.bitwise_and)
         for k in range(1, 4):
-            ts(w("GG", k, 16 * NCH, 8), w("MM"), w("KC", k, k + 1), A.is_lt)
-        ts(w("GG", 4, 16 * NCH, 8), w("MM"), 0.0, A.is_gt)
-        scan(w("XS"), w("GG"), w("CH", 1, 32 * NCH, 2))
-        new = "AL%d" % t
-        tt(w(new, 0, 28, 2), w("XS", 7, 224, 16), w("XS", 239, 448, 16), A.add)
-        tt(w(new, 1, 27, 2), w("XS", 247, 448, 16), w("XS", 15, 216, 16), A.add)
-        copy("v", w("LS%d" % t), w(new, 16, 28))
-        send(T["LR%d" % t][:], T["LS%d" % t][:], ("LS%d" % t, 0, 128, 0, 12, 1), "l%d" % t)
-        copy("v", w("LO%d" % t), w(new, 0, 16))
+            ts(w("GG", k, 5 * LC, 5), w("MS"), w("KC", k, k + 1), A.is_lt)
+        ts(w("GG", 4, 5 * LC, 5), w("MS"), 0.0, A.is_gt)
+        scan(w("XS"), w("GG"), w("NS"))
+        ts(w("LA%d" % t), w("XS", 4, 5 * LC, 5), 2.0, A.mult)
+        send(w("LR%d" % t), w("LA%d" % t, LO, LC), "l%d" % t)
+        if t + 1 < ROUNDS:
+            for half in range(2):
+                ts(w("L2", half, 2 * LO, 2), w("XS", 4, 5 * LO, 5), 2.0, A.mult)
 
     def layer(h, bs=range(4)):
         z = (("ZOc", "ZOs"), ("ZRc", "ZRs"))[h]
-        m = (NO, NR)[h]
-        return [product([("Wc", "Ws", 128 * b), ("CTc", "CTs", 128 * b)], z, 0, m) for b in bs]
+        return [product(4 * h + b, [("Wc", "Ws", 128 * b), ("CTc", "CTs", 128 * b)], z, 0, (NO, NR)[h]) for b in bs]
 
     def state(h, outs, qs, bs=range(4)):
         c0, c1 = PARTS[h]
@@ -383,88 +391,73 @@ def rank_program(g, core, T, topo):
             copy(qs[b], w("X", 4 * c0 + b, 4 * c1, 4), outs[b], 2.0 ** -6)
 
     def addresses_out():
-        copy("v", w("OAF", 0, 14), w("AL%d" % (ROUNDS - 1), 0, 14))
-        copy("v", w("OAF", 14, 24), w("LR%d" % (ROUNDS - 1), 0, 10))
+        copy("v", w("OAF", 0, LO), w("XS", 4, 5 * LO, 5))
+        copy("v", w("OAF", LO, LC), w("LR%d" % (ROUNDS - 1)), 0.5)
         turn(w("OAT"), w("OAF"))
         for k in range(8):
-            p0 = 32 * (k // 2)
-            dma("y", T.oa[k:k + 1, :], T.OAT[p0:p0 + 24, 16 * (k % 2):16 * (k % 2) + 16], [("OAT", p0, p0 + 24, 0, 32, 1)])
+            src = w("OAT", 16 * (k % 2), 16 * (k % 2) + 16, p=(32 * (k // 2), 32 * (k // 2) + LC))
+            dma("y", T.oa[k:k + 1, :], src[0], [src])
 
-    sa = score(0, 0)
-    sb = score(0, 1)
     for t in range(ROUNDS):
         last = t + 1 == ROUNDS
-        fa = unpack(("Qc%d" % t, "Qs%d" % t), "FO", 0, "ssss")
-        if t == 0:
-            bits(sa, 0)
-            edges(0)
-            bits(sb, 1)
-            edges(1)
-            for ph in range(4):
-                copy("sv"[ph % 2], w("D1", 2 * ph + 1, 768, 8), w("TAB", 192 * ph, 192 * ph + 96), w("SC"))
-                copy("vs"[ph % 2], w("D0", 2 * ph + 1, 768, 8), w("TAB", 192 * ph + 96, 192 * ph + 192), w("SC"))
-            choose(0)
-            turns(0, "EO", "CE", 32)
-        else:
-            bits(sb, 1)
-            edges(1)
-        choose(1)
-        gather("s", w("RO", 0, 240), w("TW", 8, 776), w("L2O", 0, 15))
-        gather("v", w("RR", 0, 176), w("TW", 8, 776), w("L2R", 0, 11))
-        turns(1, "ER", "CE", 32)
-        start()
-        turns(1, "RR", "CH", 128)
-        tt(view("MM", 0, 2 * NCH, 2, 0, 32), view("MA", 0, NCH, 1, 0, 32), view("MB", 0, NCH, 1, 0, 32), A.mult)
-        turns(0, "RO", "CH", 128)
-        take(fa)
-        take(unpack(("Qc%d" % t, "Qs%d" % t), "FO", 1, "ssss"))
-        carries(t)
-        take(unpack(("Ac%d" % t, "As%d" % t), "FP", 0, "ssss"))
+        fo = unpack(("Qc%d" % t, "Qs%d" % t), "FO", (2, 3, 0, 4), "ssss")
+        for q, a, b in PICKS:
+            gather(q, w("RD", 32 * a, 32 * b), w("TW", 8, 776), w("L2", 2 * a, 2 * b))
+        turn_edges(1)
+        for q, a, b in PICKS:
+            turn(v("CH", S(a, b)), w("RD", 32 * a, 32 * b))
+            if q == "v":
+                tt(w("MI", p=Q[0]), v("CE", ALL, EDGE, p=Q[0]), v("CE", ALL, EDGE + 1, p=Q[0]), A.mult)
+        take(fo[:2])
+        fp = unpack(("Ac%d" % t, "As%d" % t), "FP", (1, 5, 6, 7), "sssv")
+        carries(t, fo[2:] + fp[:3])
         for b in range(4):
-            gather("vsvs"[b], w("ZO", b, 4 * NO, 4), w("FO", C * b, C * b + C), w("LO%d" % t, 0, 14))
+            gather("vsvs"[b], w("ZO", b, 4 * NO, 4), w("FO", 2 * C * b, 2 * C * (b + 1)), w("LA%d" % t, 0, LO))
         quant("ZOc", "ZOs", "ZO", 0, NO, 0)
-        take(unpack(("Ac%d" % t, "As%d" % t), "FP", 1, "vsvs"))
         outs = layer(0)
+        take(fp[3:])
+        for b in range(4):
+            gather("svsv"[b], w("ZR", b, 4 * NR, 4), w("FP", 2 * C * b, 2 * C * (b + 1)), w("LR%d" % t))
+        quant("ZRc", "ZRs", "ZR", 0, NR, 0)
         if t == 0:
             quant("Vc", "Vs", "VB", 0, 128, 0)
         if not last:
-            ts(w("L2O", 0, 16), w("AL%d" % t, 0, 16), 2.0, A.mult)
-        for b in range(4):
-            gather("vsvs"[b], w("ZR", b, 4 * NR, 4), w("FP", C * b, C * b + C), w("LR%d" % t, 0, 10))
-        quant("ZRc", "ZRs", "ZR", 0, NR, 0)
-        outs2 = layer(1, (0, 1))
+            for half in range(2):
+                copy("v", w("L2", 2 * LO + half, 2 * LC, 2), w("LR%d" % t))
         if last:
             addresses_out()
-        state(0, outs, "svsv")
+        state(0, outs, "ssss")
         quant_x(t + 1, 0)
-        if not last:
-            send_x(t + 1, 0, NO, 0)
-            sa = score(t + 1, 0)
-            ts(w("L2R", 0, 12), w("LR%d" % t), 2.0, A.mult)
-        outs2 += layer(1, (2, 3))
         if last:
-            state(1, outs2, "svsv")
+            outs2 = layer(1)
+            state(1, outs2, "vsvs")
+            quant_x(t + 1, 1)
         else:
-            state(1, outs2, "svss", (0, 1))
+            send_x(t + 1, 0, NO, 0)
+            outs2 = layer(1, (0, 1, 2))
+            sa = score(t + 1, 0)
+            outs2 += layer(1, (3,))
+            state(1, outs2, "vsss")
             bits(sa, 0)
+            quant_x(t + 1, 1)
             edges(0)
-            choose(0)
-            state(1, outs2, "svss", (2, 3))
-            turns(0, "EO", "CE", 32)
-        quant_x(t + 1, 1)
-        if not last:
             send_x(t + 1, NO, C, 1)
             sb = score(t + 1, 1)
+            choose(0, NO)
+            bits(sb, 1)
+            edges(1)
+            turn_edges(0)
+            choose(NO, C)
 
     qc, qs = "Qc%d" % ROUNDS, "Qs%d" % ROUNDS
     for h, (c0, c1) in enumerate(PARTS):
-        out = product([("Vc", "Vs", 0)], (qc, qs), c0, c1)
-        dma("ys"[h], T.oc[:, 4 * c0:4 * c1], T[qc][:, c0:c1].bitcast(dt.uint8), [(qc, 0, 128, c0, c1, 1)])
+        out = product(h, [("Vc", "Vs", 0)], (qc, qs), c0, c1)
+        dma("ys"[h], T.oc[:, 4 * c0:4 * c1], T[qc][:, c0:c1].bitcast(dt.uint8), [w(qc, c0, c1)])
         copy("sv"[h], w("Y", c0, c1), out)
-        dma("ys"[h], T.y[:, c0:c1], T.Y[:, c0:c1], [("Y", 0, 128, c0, c1, 1)])
+        dma("ys"[h], T.y[:, c0:c1], T.Y[:, c0:c1], [w("Y", c0, c1)])
     for k in range(4):
-        dma("y", T.osc[4 * k:4 * k + 4, :], T[qs][32 * k:32 * k + 4, :], [(qs, 0, 128, 0, C, 1)])
+        dma("y", T.osc[4 * k:4 * k + 4, :], T[qs][32 * k:32 * k + 4, :], [w(qs)])
 
     for s in sorted(count):
-        if need_end.get(s, 0) < count[s]:
+        if waited.get(s, 0) < count[s]:
             g.wait_ge(T.sem[s], count[s])

@@ -6,25 +6,25 @@ C, NO, NR, ROUNDS = 384, 224, 160, 3
 PARTS = ((0, NO), (NO, C))
 LC, LO = C // 16, NO // 16
 A0, B0 = 15, 3
-CLOSE = [2 ** (A0 + k) for k in range(4)]
-WIDE = [2 ** (B0 + 4 * k) for k in range(4)]
-WORD, DIFF, ADDR, EDGE = 4, 5, 9, 10
+CLOSE = sum(2 ** (A0 + k) for k in range(4))
+WIDE = sum(2 ** (B0 + 4 * k) for k in range(4))
+WORD, DIFF, ADDR, FIRST, EDGE = 4, 5, 9, 10, 14
+N5 = 5 * LC
 
 _F, _I, _B, _U = "float32", "int32", "bfloat16", "uint16"
 SCRATCH = {
     "NX": ("sbuf", [128, 192], _I), "NT": ("sbuf", [128, 12, 4, 4], _I), "CI": ("sbuf", [128, 192], _I), "NI": ("sbuf", [128, 12, 4, 4], _I),
-    "U4": ("sbuf", [128, 192], _F), "UA": ("sbuf", [128, 192], _F), "V2": ("sbuf", [128, 192], _F), "UB": ("sbuf", [128, 192], _F),
-    "SE": ("sbuf", [128, 192], _F), "SO": ("sbuf", [128, 192], _F), "HE": ("sbuf", [128, 192], _F), "HO": ("sbuf", [128, 192], _F),
+    "U4": ("sbuf", [128, 192], _F), "UA": ("sbuf", [128, 12, 4, 4], _F), "V2": ("sbuf", [128, 12, 4, 4], _F), "UM": ("sbuf", [128, 192], _I),
+    "UF": ("sbuf", [128, 96], _F), "SW": ("sbuf", [128, 192], _F), "SF": ("sbuf", [128, 96], _F), "HR": ("sbuf", [128, 192], _F),
     "TT": ("sbuf", [128, 12, 4, 16], _F), "ZZ": ("sbuf", [128, C], _F),
     "D0": ("sbuf", [128, 768], _F), "D1": ("sbuf", [128, 768], _F), "TW": ("sbuf", [128, 776], _F),
     "RD": ("sbuf", [128, 2 * C], _F), "CH": ("sbuf", [128, LC, 32], _F),
     "ED": ("sbuf", [128, LC, 2, 16], _B), "CE": ("sbuf", [128, LC, 32], _B),
-    "MI": ("sbuf", [128, LC], _I), "M1": ("sbuf", [128, LC], _I), "MS": ("sbuf", [128, LC], _I), "YY": ("sbuf", [128, 5, LC], _I),
-    "Y4": ("sbuf", [128, 4 * LC], _I), "Z4": ("sbuf", [128, 4 * LC], _I), "ZF": ("sbuf", [128, 4 * LC], _F), "PP": ("sbuf", [128, 4 * LC], _F),
-    "HM": ("sbuf", [128, 4 * LC], _F), "WS": ("sbuf", [128, LC], _F),
-    "GG": ("sbuf", [128, 5 * LC], _F), "NS": ("sbuf", [128, 5 * LC], _F), "XS": ("sbuf", [128, 5 * LC], _F),
+    "M1": ("sbuf", [128, LC], _I), "YY": ("sbuf", [128, 3, LC], _I),
+    "Y5": ("sbuf", [128, N5], _I), "Z5": ("sbuf", [128, N5], _I), "YS": ("sbuf", [128, N5], _I), "FA": ("sbuf", [128, N5], _I),
+    "WS": ("sbuf", [128, LC], _F), "GG": ("sbuf", [128, N5], _I), "NS": ("sbuf", [128, N5], _F), "XS": ("sbuf", [128, N5], _F),
     "PI": ("sbuf", [128, 1], _I), "P15": ("sbuf", [128, 1], _I), "PUI": ("sbuf", [128, 1], _I), "PU": ("sbuf", [128, 1], _F),
-    "IDL": ("sbuf", [128, 1], _F), "SCP": ("sbuf", [128, 1], _F), "KC": ("sbuf", [128, 4], _F), "EE": ("sbuf", [128, 2], _F),
+    "IDL": ("sbuf", [128, 1], _F), "EE": ("sbuf", [128, 1], _F),
     "LP": ("sbuf", [128, 8], _I), "LPU": ("sbuf", [128, 8], _U),
     "ALI": ("sbuf", [128, LC], _I), "L2": ("sbuf", [128, 2 * LC], _U), "OAF": ("sbuf", [128, 32], _F), "OAT": ("sbuf", [128, 32], _F),
     "CT": ("sbuf", [128, 516], _B), "CTc": ("sbuf", [128, 512], CODES), "CTs": ("sbuf", [128, 512], "uint8"),
@@ -228,31 +228,23 @@ def rank_program(g, core, T, topo):
     mark(w("CT", 3, 515, 4), [[-1, 128]], 64.0, 0)
     iota(w("LP"), [[16, 8]], 0, 0)
     iota(v("TT", S(0, 6), ALL, ADDR), [[128, 3], [0, 2], [1, 4]], 0, 4, True)
-    mark(w("EE", 0, 1), [[0, 1]], 3.0 * CLOSE[0], -EDGE)
-    mark(w("EE", 1, 2), [[0, 1]], 1.0 * CLOSE[0], -EDGE)
-    const(w("HO"), 16)
-    const(w("HE"), 2)
-    const(v("TT", ALL, ALL, S(EDGE, 16)), 0)
+    mark(w("EE"), [[0, 1]], 3.0, -EDGE)
+    const(w("HR"), 2)
+    const(v("TT", ALL, ALL, S(FIRST, 16)), 0)
+    const(w("HR", 0, 96, p=(64, 128)), 16)
+    const(w("HR", 96, 192, p=Q[0]), 16)
     const(v("TT", ALL, ALL, S(0, 4)), 0)
-    const(w("HO", 0, 192, 4), 0)
-    const(w("HE", 0, 192, 4), 0)
+    const(w("HR", 0, 192, 4), 0)
     const(v("TT", S(6, 12), ALL, ADDR), 0)
     for k in range(1, 4):
         a = v("TT", S(0, 6), ALL, ADDR, p=Q[k])
         act(a, a, ACT.Identity, 1.0, -128.0 * k)
-    const(w("D0", 0, 768, 2), 0)
     ts(w("P15"), w("PI"), 15, A.bitwise_and)
     ts(w("PUI"), w("PI"), 4, A.logical_shift_right, 1, A.bitwise_and)
     for b in range(4):
         quant("CTc", "CTs", "CT", 128 * b, 128 * b + 128, 3 - b)
     ts(w("LPU", 0, 1), w("P15"), 16.0, A.mult, 1.0 - 16.0 * EDGE, A.add)
     copy("v", w("LPU", 1, 8), w("LP", 1, 8))
-    copy("v", w("PU"), w("PUI"))
-    same = (sum(WIDE[k] / CLOSE[k] for k in range(4)), sum(CLOSE[k] / WIDE[k] for k in range(4)))
-    for p, word in (((0, 64), same[0]), (Q[2], same[1]), (Q[3], same[0])):
-        ts(w("IDL", p=p), w("PUI", p=p), -word, A.mult, word, A.add)
-    fill(w("Z4"), 0)
-    fill(w("OAF"), 0.0)
 
     def send_x(t, c0, c1, h):
         send(w("Ac%d" % t, c0, c1), w("Qc%d" % t, c0, c1), "q%d%d" % (t, h), True)
@@ -273,7 +265,7 @@ def rank_program(g, core, T, topo):
     def edges(h):
         c0, c1 = PARTS[h]
         for half in range(2):
-            act(v("ED", S(c0 // 16, c1 // 16), half, p=Q[0]), w("D1", 2 * c0, 2 * c1, 2, p=Q[0]), ACT.Identity, w("EE", 0, 1, p=Q[0]), w("EE", 1, 2, p=Q[0]))
+            act(v("ED", S(c0 // 16, c1 // 16), half, p=Q[0]), w("D1", 2 * c0, 2 * c1, 2, p=Q[0]), ACT.Identity, w("EE", p=Q[0]), 1.0)
 
     def turn_edges(h):
         c = S(PARTS[h][0] // 16, PARTS[h][1] // 16)
@@ -289,50 +281,56 @@ def rank_program(g, core, T, topo):
     ts(w("U4"), w("CI"), 4.0, A.mult, -8.0, A.add)
     op("v", lambda e: e.tensor_copy(T.Pc[:, 0:128].bitcast(dt.uint32), T.Uc[:, 0:128].bitcast(dt.uint32).indirect(T.LPU[:, 0:8])), [w("Uc"), w("LPU")], [w("Pc")])
     gather("s", w("Ps"), w("Us"), w("LPU"))
-    tt(w("UA"), w("CI"), w("U4"), A.max)
-    act(w("V2"), w("UA"), ACT.Square)
-    act(w("UB"), w("V2"), ACT.Square)
-    tt(v("TT", ALL, ALL, S(DIFF, DIFF + 3)), v("NI", ALL, ALL, S(0, 3)), v("NI", ALL, ALL, S(1, 4)), A.subtract)
-    scan(w("SO"), w("HO"), w("UA"))
+    even, odd = S(0, 12, 2), S(1, 12, 2)
+    tt(v("UA"), w("CI"), w("U4"), A.max)
+    act(v("V2"), v("UA"), ACT.Square)
+    act(w("UM", 0, 96, p=(64, 128)), v("UA", even, p=(64, 128)), ACT.Relu, 2.0, -1.0)
+    copy("s", w("UM", 96, 192, p=Q[0]), v("UA", odd, p=Q[0]))
+    act(w("UM", 0, 96, p=(0, 64)), v("V2", even, p=(0, 64)), ACT.Square, (16.0 / 15.0) ** 0.5)
+    for p in (Q[1], (64, 128)):
+        act(w("UM", 96, 192, p=p), v("V2", odd, p=p), ACT.Square)
+    act(w("UF", p=Q[0]), v("V2", even, p=Q[0]), ACT.Square)
+    for k in (1, 2):
+        copy("s", v("TT", even, ALL, S(0, 4), p=Q[k]), v("UA", even, p=Q[k]))
+    for k in range(3):
+        tt(v("TT", ALL, ALL, DIFF + k), v("NI", ALL, ALL, 3 - k), v("NI", ALL, ALL, 2 - k), A.subtract)
     for b in range(2):
-        tt(v("TT", S(6 * b, 6 * b + 6), ALL, DIFF + 3), v("NI", S(6 * b, 6 * b + 6), ALL, 3), v("TT", S(0, 6), ALL, ADDR), A.subtract)
-    scan(w("SE"), w("HE"), w("UB"))
-    copy("s", v("TT", ALL, ALL, S(0, 4), p=Q[1]), w("UA", p=Q[1]), float(CLOSE[0]))
-    for k in (0, 2):
-        copy("s", v("TT", ALL, ALL, WORD, p=Q[k]), w("SO", 3, 192, 4, p=Q[k]), CLOSE[0] / WIDE[3])
-    copy("s", v("TT", ALL, ALL, S(0, 4), p=Q[2]), w("UB", p=Q[2]), float(WIDE[0]))
+        tt(v("TT", S(6 * b, 6 * b + 6), ALL, DIFF + 3), v("NI", S(6 * b, 6 * b + 6), ALL, 0), v("TT", S(0, 6), ALL, ADDR), A.subtract)
     quant_x(0, 0)
     sa = score(0, 0)
-    for k in (1, 3):
-        copy("s", v("TT", ALL, ALL, WORD, p=Q[k]), w("SE", 3, 192, 4, p=Q[k]), WIDE[0] / CLOSE[3])
-    for ph in range(4):
-        copy("sv"[ph % 2], v("TT", S(0, 12, 2), ph, WORD, p=Q[0]), w("SE", 4 * ph + 3, 192, 32, p=Q[0]), WIDE[0] / CLOSE[3])
     quant_x(0, 1)
     sb = score(0, 1)
     send_x(0, 0, C, 0)
+    scan(w("SW"), w("HR"), w("UM"))
+    scan(w("SF", p=Q[0]), w("HR", 0, 96, p=Q[0]), w("UF", p=Q[0]))
+    const(w("D0", 0, 768, 2), 0)
     bits(sa, 0)
-    tt(v("TT", S(6, 12), ALL, S(0, ADDR)), v("TT", S(6, 12), ALL, S(0, ADDR)), v("TT", S(0, 6), ALL, S(0, ADDR)), A.subtract)
+    copy("v", v("TT", even, ALL, WORD), w("SW", 3, 96, 4))
+    copy("v", v("TT", odd, ALL, WORD), w("SW", 99, 192, 4))
+    copy("v", v("TT", even, ALL, FIRST, p=Q[0]), w("SF", 3, 96, 4, p=Q[0]))
     edges(0)
-    for ph in range(4):
-        turn(w("D1", 2 * ph + 1, 768, 8), v("TT", S(0, 6), ph))
     bits(sb, 1)
     edges(1)
+    for r, p in ((S(0, ADDR), (0, 128)), (FIRST, Q[0])):
+        tt(v("TT", S(6, 12), ALL, r, p=p), v("TT", S(6, 12), ALL, r, p=p), v("TT", S(0, 6), ALL, r, p=p), A.subtract)
+    for ph in range(4):
+        turn(w("D1", 2 * ph + 1, 768, 8), v("TT", S(0, 6), ph))
     for ph in range(4):
         turn(w("D0", 2 * ph + 1, 768, 8), v("TT", S(6, 12), ph))
     for half in range(2):
         ts(w("L2", half, 2 * LC, 2), w("ALI"), 2.0, A.mult)
+    copy("v", w("PU"), w("PUI"))
     choose(0, C)
     turn_edges(0)
-    const(w("HM"), 2)
-    const(w("GG", 0, 5 * LC, 5), 0)
-    const(w("SCP"), 1.0 / CLOSE[3])
-    for k in range(1, 4):
-        const(w("KC", k, k + 1), WIDE[k])
-    const(w("HM", p=Q[2]), 16)
-    const(w("SCP", p=Q[2]), 1.0 / WIDE[3])
-    for k in range(1, 4):
-        const(w("KC", k, k + 1, p=Q[2]), CLOSE[k])
-    const(w("HM", 0, 4 * LC, 4), 0)
+    const(w("FA", p=Q[1]), 2)
+    const(w("FA", p=Q[3]), 16)
+    const(w("GG", 0, N5, 5), 0)
+    const(w("Y5", 4, N5, 5), 0)
+    const(w("OAF"), 0)
+    const(w("FA", 0, N5, 5), 0)
+    same = (sum(sum(16 ** i for i in range(e + 1)) * 2 ** (3 - e) for e in range(4)), sum((2 ** (e + 1) - 1) * 16 ** (3 - e) for e in range(4)))
+    for p, word in (((0, 64), same[0]), ((64, 128), same[1])):
+        act(w("IDL", p=p), w("PU", p=p), ACT.Identity, -float(word), float(word))
 
     def unpack(src, dst, banks, qs):
         outs = [product(banks[b], [("CTc", "CTs", 128 * b)], src, 0, C) for b in range(4)]
@@ -343,37 +341,42 @@ def rank_program(g, core, T, topo):
             copy(q, out, ps, 2.0 ** -6)
 
     def carries(t, gaps):
-        close, wide = sum(CLOSE), sum(WIDE)
         y = lambda i, p: v("YY", i, p=p)
+        m = lambda p: w("FA", 4, N5, 5, p=p)
+        AND, SHR = A.bitwise_and, A.logical_shift_right
+
+        def through(e):
+            tt(w("Y5", e, N5, 5, p=Q[3]), w("Z5", e, N5, 5, p=Q[2]), w("WS", p=Q[3]), A.mult)
+
+        def flags(src, first, step, p, ks):
+            for k in ks:
+                ts(w("GG", 4 - k, N5, 5, p=p), src, first + step * k, SHR, 1, AND)
+        tt(y(0, Q[0]), v("CH", ALL, FIRST, p=Q[0]), m(Q[0]), A.mult)
         for e in range(4):
-            tt(w("Y4", e, 4 * LC, 4, p=(0, 96)), v("CH", ALL, e, p=(0, 96)), v("CH", ALL, 16 + WORD, p=(0, 96)), A.mult)
+            tt(w("Y5", e, N5, 5, p=(0, 96)), v("CH", ALL, e, p=(0, 96)), v("CH", ALL, 16 + WORD, p=(0, 96)), A.mult)
         act(w("WS"), v("CH", ALL, WORD), ACT.Identity, w("PU"), w("IDL"))
-        tt(y(0, Q[0]), v("CH", ALL, WORD, p=Q[0]), w("MI", p=Q[0]), A.mult)
-        ts(w("Z4", p=Q[1]), w("Y4", p=Q[1]), wide, A.bitwise_and)
-        ts(w("Z4", p=Q[2]), w("Y4", p=Q[2]), close, A.bitwise_and)
-        ts(w("M1", p=Q[0]), y(0, Q[0]), wide, A.bitwise_and)
-        ts(w("ZF", p=(0, 96)), w("Z4", p=(0, 96)), w("SCP", p=(0, 96)), A.mult)
+        ts(w("M1", p=Q[0]), y(0, Q[0]), WIDE, AND)
+        ts(w("Z5", p=(0, 96)), w("Y5", p=(0, 96)), WIDE, AND)
         tt(y(1, Q[0]), v("CH", ALL, 16 + WORD, p=Q[0]), w("M1", p=Q[0]), A.mult)
-        scan(w("PP", p=(0, 96)), w("HM", p=(0, 96)), w("ZF", p=(0, 96)))
-        ts(w("MI", p=Q[1]), y(1, Q[0]), close, A.bitwise_and)
+        through(0)
+        ts(m(Q[1]), y(1, Q[0]), CLOSE, AND, A0, SHR)
+        for e in range(1, 4):
+            through(e)
         copy("s", w("NS"), v("CH", ALL, S(16 + DIFF, 16 + ADDR + 1)))
         take(gaps[:1])
         for k in range(4):
             p = (32 * k, 32 * k + 16)
             copy("s", w("NS", p=p), v("CH", ALL, S(DIFF, ADDR + 1), p=p))
         take(gaps[1:])
-        tt(y(2, Q[1]), w("PP", 3, 4 * LC, 4, p=Q[1]), w("MI", p=Q[1]), A.mult)
-        ts(w("MI", p=Q[2]), y(2, Q[1]), wide, A.bitwise_and)
-        tt(y(3, Q[2]), w("PP", 3, 4 * LC, 4, p=Q[2]), w("MI", p=Q[2]), A.mult)
-        tt(y(4, (0, 96)), w("WS", p=(0, 96)), w("MI", p=(0, 96)), A.mult)
-        ts(w("MI", p=Q[3]), y(3, Q[2]), close, A.bitwise_and)
-        ts(w("MS", p=(0, 64)), y(4, (0, 64)), wide, A.bitwise_and)
-        tt(y(4, Q[3]), w("WS", p=Q[3]), w("MI", p=Q[3]), A.mult)
-        ts(w("MS", p=Q[2]), y(4, Q[2]), close, A.bitwise_and)
-        ts(w("MS", p=Q[3]), y(4, Q[3]), wide, A.bitwise_and)
-        for k in range(1, 4):
-            ts(w("GG", k, 5 * LC, 5), w("MS"), w("KC", k, k + 1), A.is_lt)
-        ts(w("GG", 4, 5 * LC, 5), w("MS"), 0.0, A.is_gt)
+        scan(w("YS", p=Q[1]), w("FA", p=Q[1]), w("Z5", p=Q[1]))
+        ts(w("Z5", p=Q[3]), w("Y5", p=Q[3]), CLOSE, AND, A0, SHR)
+        tt(y(2, (0, 64)), w("WS", p=(0, 64)), m((0, 64)), A.mult)
+        ts(m(Q[3]), w("YS", 4, N5, 5, p=Q[1]), WIDE << 3, AND, 3, SHR)
+        flags(y(2, (0, 64)), B0, 4, (0, 64), range(3))
+        scan(w("YS", p=Q[3]), w("FA", p=Q[3]), w("Z5", p=Q[3]))
+        tt(w("YS", 4, N5, 5, p=Q[2]), w("WS", p=Q[2]), m(Q[3]), A.mult)
+        flags(y(2, (0, 64)), B0, 4, (0, 64), (3,))
+        flags(w("YS", 4, N5, 5, p=(64, 128)), A0, 1, (64, 128), range(4))
         scan(w("XS"), w("GG"), w("NS"))
         ts(w("LA%d" % t), w("XS", 4, 5 * LC, 5), 2.0, A.mult)
         send(w("LR%d" % t), w("LA%d" % t, LO, LC), "l%d" % t)
@@ -407,7 +410,7 @@ def rank_program(g, core, T, topo):
         for q, a, b in PICKS:
             turn(v("CH", S(a, b)), w("RD", 32 * a, 32 * b))
             if q == "v":
-                tt(w("MI", p=Q[0]), v("CE", ALL, EDGE, p=Q[0]), v("CE", ALL, EDGE + 1, p=Q[0]), A.mult)
+                tt(w("FA", 4, N5, 5, p=Q[0]), v("CE", ALL, EDGE, p=Q[0]), v("CE", ALL, EDGE + 1, p=Q[0]), A.mult)
         take(fo[:2])
         fp = unpack(("Ac%d" % t, "As%d" % t), "FP", (1, 5, 6, 7), "sssv")
         carries(t, fo[2:] + fp[:3])
@@ -434,10 +437,9 @@ def rank_program(g, core, T, topo):
             quant_x(t + 1, 1)
         else:
             send_x(t + 1, 0, NO, 0)
-            outs2 = layer(1, (0, 1, 2))
+            outs2 = layer(1)
             sa = score(t + 1, 0)
-            outs2 += layer(1, (3,))
-            state(1, outs2, "vsss")
+            state(1, outs2, "ssss")
             bits(sa, 0)
             quant_x(t + 1, 1)
             edges(0)

@@ -1,3 +1,4 @@
+import math
 import numpy as np
 from concourse.mybir import dt, AluOpType, ActivationFunctionType
 
@@ -8,23 +9,30 @@ LC, LO = C // 16, NO // 16
 A0, B0 = 15, 3
 CLOSE = sum(2 ** (A0 + k) for k in range(4))
 WIDE = sum(2 ** (B0 + 4 * k) for k in range(4))
-WORD, DIFF, ADDR, FIRST, EDGE = 4, 5, 9, 10, 14
+WORD, DIFF, ADDR, EDGE = 4, 5, 9, 10
 N5 = 5 * LC
+UP = 512.0
+LIFT = 32.0
+EDGE_ROWS = ((-LIFT, LIFT), ((LIFT ** 2 - 1) / LIFT ** 3, 1 / LIFT ** 3), (3.0, 1.0), (-LIFT, LIFT), (LIFT - 1, 1.0), (1.0, 1.0))
+LN2 = math.log(2.0)
+ONE_CLOSE = (math.log(2.03), math.log(1.005 / 2.03))
+ONE_WIDE = (4 * LN2, -4 * LN2 + 3e-5)
+ALL_WIDE = (4 * LN2, math.log(1 / 15))
+NOT_CLOSE = (-LN2, 4 * LN2 + 3e-5)
 
 _F, _I, _B, _U = "float32", "int32", "bfloat16", "uint16"
 SCRATCH = {
-    "NX": ("sbuf", [128, 192], _I), "NT": ("sbuf", [128, 12, 4, 4], _I), "CI": ("sbuf", [128, 192], _I), "NI": ("sbuf", [128, 12, 4, 4], _I),
-    "U4": ("sbuf", [128, 192], _F), "UA": ("sbuf", [128, 12, 4, 4], _F), "V2": ("sbuf", [128, 12, 4, 4], _F), "UM": ("sbuf", [128, 192], _I),
-    "UF": ("sbuf", [128, 96], _F), "SW": ("sbuf", [128, 192], _F), "SF": ("sbuf", [128, 96], _F), "HR": ("sbuf", [128, 192], _F),
-    "TT": ("sbuf", [128, 12, 4, 16], _F), "ZZ": ("sbuf", [128, C], _F),
-    "D0": ("sbuf", [128, 768], _F), "D1": ("sbuf", [128, 768], _F), "TW": ("sbuf", [128, 776], _F),
-    "RD": ("sbuf", [128, 2 * C], _F), "CH": ("sbuf", [128, LC, 32], _F),
+    "NX": ("sbuf", [128, 192], _I), "NT": ("sbuf", [128, 12, 4, 4], _I), "CI": ("sbuf", [128, 12, 4, 4], _I), "NI": ("sbuf", [128, 12, 4, 4], _I),
+    "UM": ("sbuf", [128, 192], _I), "SW": ("sbuf", [128, 192], _F), "HR": ("sbuf", [128, 192], _I), "XP": ("sbuf", [128, 8], _F),
+    "TT": ("sbuf", [128, 12, 4, 16], _I), "ZZ": ("sbuf", [128, 192], _F),
+    "D0": ("sbuf", [128, 768], _I), "D1": ("sbuf", [128, 768], _I), "TW": ("sbuf", [128, 776], _F),
+    "RD": ("sbuf", [128, 2 * C], _U), "CH": ("sbuf", [128, LC, 32], _U), "NE": ("sbuf", [128, N5], _F),
     "ED": ("sbuf", [128, LC, 2, 16], _B), "CE": ("sbuf", [128, LC, 32], _B),
-    "M1": ("sbuf", [128, LC], _I), "YY": ("sbuf", [128, 3, LC], _I),
+    "YY": ("sbuf", [128, 2, LC], _I), "Z0": ("sbuf", [128, N5], _I), "FB": ("sbuf", [128, N5], _F), "MM": ("sbuf", [128, N5], _I),
     "Y5": ("sbuf", [128, N5], _I), "Z5": ("sbuf", [128, N5], _I), "YS": ("sbuf", [128, N5], _I), "FA": ("sbuf", [128, N5], _I),
     "WS": ("sbuf", [128, LC], _F), "GG": ("sbuf", [128, N5], _I), "NS": ("sbuf", [128, N5], _F), "XS": ("sbuf", [128, N5], _F),
     "PI": ("sbuf", [128, 1], _I), "P15": ("sbuf", [128, 1], _I), "PUI": ("sbuf", [128, 1], _I), "PU": ("sbuf", [128, 1], _F),
-    "IDL": ("sbuf", [128, 1], _F), "EE": ("sbuf", [128, 1], _F),
+    "IDL": ("sbuf", [128, 1], _F), "EE": ("sbuf", [128, 2], _F), "PE": ("sbuf", [128, 2], _I),
     "LP": ("sbuf", [128, 8], _I), "LPU": ("sbuf", [128, 8], _U),
     "ALI": ("sbuf", [128, LC], _I), "L2": ("sbuf", [128, 2 * LC], _U), "OAF": ("sbuf", [128, 32], _F), "OAT": ("sbuf", [128, 32], _F),
     "CT": ("sbuf", [128, 516], _B), "CTc": ("sbuf", [128, 512], CODES), "CTs": ("sbuf", [128, 512], "uint8"),
@@ -49,7 +57,8 @@ for _t in range(ROUNDS):
 for _t in range(8):
     SCRATCH["pb%d" % _t] = ("psum", [128, 512], _F)
 SEMAPHORES = ["cv", "cs", "ct", "cg", "sent"] + ["d%d" % i for i in range(32)] + ["q%d%d" % (t, h) for t in range(ROUNDS) for h in range(2)] + ["l%d" % t for t in range(ROUNDS)]
-PICKS = (("v", 0, 8), ("s", 8, 16), ("s", 16, 24))
+PICKS = (("v", 0, 10), ("s", 10, 17), ("s", 17, 24))
+EARLY = 176
 S = slice
 ALL = slice(None)
 
@@ -208,47 +217,55 @@ def rank_program(g, core, T, topo):
     for t in range(ROUNDS):
         for h, (c0, c1) in enumerate(PARTS):
             for name in ("Ac%d" % t, "As%d" % t):
-                lands(w(name, c0, c1), "q%d%d" % (t, h if t else 0), 2 * n_in)
+                lands(w(name, c0, c1), "q%d%d" % (t, h), 2 * n_in)
         lands(w("LR%d" % t), "l%d" % t, n_in)
     Q = [(32 * k, 32 * k + 32) for k in range(4)]
 
     load("y", "NX", T.nx[:])
-    load("s", "UU", T.u[:])
+    load("s", "ALI", T.al[:])
+    load("y", "UU", T.u[:])
     load("y", "X", T.x[:, 0:4 * NO], 0, 4 * NO)
     load("y", "X", T.x[:, 4 * NO:4 * C], 4 * NO, 4 * C)
-    load("y", "ALI", T.al[:])
-    load("y", "Wc", T.wc[:], after=[w("X")])
-    load("y", "Ws", T.ws[:])
-    load("y", "VB", T.v[:])
 
-    fill(w("CT"), 0.0)
+    even, odd = S(0, 12, 2), S(1, 12, 2)
     fill(w("ZZ"), 0.0)
+    fill(w("CT"), 0.0)
     fill(w("EE"), 1.0)
     iota(w("PI"), [[1, 1]], 0, 1)
-    mark(w("CT", 3, 515, 4), [[-1, 128]], 64.0, 0)
     iota(w("LP"), [[16, 8]], 0, 0)
-    iota(v("TT", S(0, 6), ALL, ADDR), [[128, 3], [0, 2], [1, 4]], 0, 4, True)
-    mark(w("EE"), [[0, 1]], 3.0, -EDGE)
-    const(w("HR"), 2)
-    const(v("TT", ALL, ALL, S(FIRST, 16)), 0)
-    const(w("HR", 0, 96, p=(64, 128)), 16)
-    const(w("HR", 96, 192, p=Q[0]), 16)
-    const(v("TT", ALL, ALL, S(0, 4)), 0)
-    const(w("HR", 0, 192, 4), 0)
-    const(v("TT", S(6, 12), ALL, ADDR), 0)
+    mark(w("CT", 3, 515, 4), [[-1, 128]], 64.0, 0)
+    iota(v("TT", S(0, 6), ALL, ADDR), [[128, 3], [0, 2], [1, 4]], 0, 4)
+    for k, row in enumerate(EDGE_ROWS):
+        for c in range(2):
+            if row[c] != 1.0:
+                mark(w("EE", c, c + 1), [[0, 1]], row[c], -(EDGE + k))
+    act(w("HR"), w("ZZ"), ACT.Exp, 1.0, LN2 + 3e-5)
     for k in range(1, 4):
         a = v("TT", S(0, 6), ALL, ADDR, p=Q[k])
         act(a, a, ACT.Identity, 1.0, -128.0 * k)
-    ts(w("P15"), w("PI"), 15, A.bitwise_and)
-    ts(w("PUI"), w("PI"), 4, A.logical_shift_right, 1, A.bitwise_and)
-    for b in range(4):
-        quant("CTc", "CTs", "CT", 128 * b, 128 * b + 128, 3 - b)
-    ts(w("LPU", 0, 1), w("P15"), 16.0, A.mult, 1.0 - 16.0 * EDGE, A.add)
-    copy("v", w("LPU", 1, 8), w("LP", 1, 8))
+    const(w("HR", 0, 96, p=(64, 128)), 16)
+    const(w("HR", 96, 192, p=Q[0]), 16)
 
-    def send_x(t, c0, c1, h):
-        send(w("Ac%d" % t, c0, c1), w("Qc%d" % t, c0, c1), "q%d%d" % (t, h), True)
-        send(w("As%d" % t, c0, c1), w("Qs%d" % t, c0, c1), "q%d%d" % (t, h))
+    def quant_ct(b):
+        quant("CTc", "CTs", "CT", 128 * b, 128 * b + 128, 3 - b)
+    ts(w("P15"), w("PI"), 15, A.bitwise_and)
+    ts(w("PE", 0, 1), w("PI"), 32.0, A.is_ge)
+    ts(w("PUI"), w("PI"), 4, A.logical_shift_right, 1, A.bitwise_and)
+    ts(w("PE", 1, 2), w("P15"), EDGE + 3.0, A.is_ge, 16.0, A.mult)
+    ts(w("LP", 0, 1), w("P15"), float(EDGE), A.is_ge)
+    for k, (low, high) in enumerate(((ONE_CLOSE, ONE_WIDE), (ONE_WIDE, ONE_CLOSE))):
+        for i in range(2):
+            ts(w("XP", 2 * k + i, 2 * k + i + 1), w("PE", 0, 1), high[i] - low[i], A.mult, low[i], A.add)
+    tt(w("LP", 0, 1), w("LP", 0, 1), w("PE", 1, 2), A.add)
+    copy("v", w("PU"), w("PUI"))
+    quant_ct(0)
+    copy("v", w("LPU"), w("LP"))
+    for half in range(2):
+        ts(w("L2", half, 2 * LC, 2), w("ALI"), 2.0, A.mult)
+
+    def send_x(t, c0, c1):
+        send(w("Ac%d" % t, c0, c1), w("Qc%d" % t, c0, c1), "q%d%d" % (t, c0 > 0), True)
+        send(w("As%d" % t, c0, c1), w("Qs%d" % t, c0, c1), "q%d%d" % (t, c0 > 0))
 
     def quant_x(t, h):
         c0, c1 = PARTS[h]
@@ -265,7 +282,7 @@ def rank_program(g, core, T, topo):
     def edges(h):
         c0, c1 = PARTS[h]
         for half in range(2):
-            act(v("ED", S(c0 // 16, c1 // 16), half, p=Q[0]), w("D1", 2 * c0, 2 * c1, 2, p=Q[0]), ACT.Identity, w("EE", p=Q[0]), 1.0)
+            act(v("ED", S(c0 // 16, c1 // 16), half, p=Q[0]), w("D1", 2 * c0, 2 * c1, 2, p=Q[0]), ACT.Identity, w("EE", 0, 1, p=Q[0]), w("EE", 1, 2, p=Q[0]))
 
     def turn_edges(h):
         c = S(PARTS[h][0] // 16, PARTS[h][1] // 16)
@@ -275,108 +292,121 @@ def rank_program(g, core, T, topo):
         scan(w("TW", 7 + 2 * c0, 7 + 2 * c1), w("D0", 2 * c0, 2 * c1), w("D1", 2 * c0, 2 * c1))
 
     turn(v("NT"), w("NX"))
-    quant("Uc", "Us", "UU", 0, 128, 0)
-    ts(w("CI"), v("NT"), 9, A.logical_shift_right)
+    quant_ct(1)
+    ts(v("CI"), v("NT"), 9, A.logical_shift_right)
     ts(v("NI"), v("NT"), 511, A.bitwise_and)
-    ts(w("U4"), w("CI"), 4.0, A.mult, -8.0, A.add)
-    op("v", lambda e: e.tensor_copy(T.Pc[:, 0:128].bitcast(dt.uint32), T.Uc[:, 0:128].bitcast(dt.uint32).indirect(T.LPU[:, 0:8])), [w("Uc"), w("LPU")], [w("Pc")])
-    gather("s", w("Ps"), w("Us"), w("LPU"))
-    even, odd = S(0, 12, 2), S(1, 12, 2)
-    tt(v("UA"), w("CI"), w("U4"), A.max)
-    act(v("V2"), v("UA"), ACT.Square)
-    act(w("UM", 0, 96, p=(64, 128)), v("UA", even, p=(64, 128)), ACT.Relu, 2.0, -1.0)
-    copy("s", w("UM", 96, 192, p=Q[0]), v("UA", odd, p=Q[0]))
-    act(w("UM", 0, 96, p=(0, 64)), v("V2", even, p=(0, 64)), ACT.Square, (16.0 / 15.0) ** 0.5)
-    for p in (Q[1], (64, 128)):
-        act(w("UM", 96, 192, p=p), v("V2", odd, p=p), ACT.Square)
-    act(w("UF", p=Q[0]), v("V2", even, p=Q[0]), ACT.Square)
-    for k in (1, 2):
-        copy("s", v("TT", even, ALL, S(0, 4), p=Q[k]), v("UA", even, p=Q[k]))
+    for p, (scale, bias) in (((0, 64), ALL_WIDE), ((64, 128), NOT_CLOSE)):
+        act(w("UM", 0, 96, p=p), v("CI", even, p=p), ACT.Exp, scale, bias)
+    const(w("HR", 0, 192, 4), 0)
+    for k, (out, half) in enumerate(((w("UM", 96, 192), odd), (v("TT", even, ALL, S(0, 4)), even))):
+        act(out, v("CI", half), ACT.Exp, w("XP", 2 * k, 2 * k + 1), w("XP", 2 * k + 1, 2 * k + 2))
+
+    def later():
+        const(v("TT", odd, ALL, S(0, 4)), 0)
+        const(v("TT", S(6, 12), ALL, ADDR), 0)
+        for b in range(2):
+            const(v("TT", S(6 * b, 6 * b + 6), ALL, S(EDGE, 16)), 0)
+        for b in range(2):
+            const(w("D0", C * b, C * b + C, 2), 0)
+
+    def latest():
+        const(w("FA", p=Q[1]), 2)
+        const(w("FA", p=Q[3]), 16)
+        const(w("GG", 0, N5, 5), 0)
+        const(w("Y5", 4, N5, 5), 0)
+        const(w("FB", 0, N5, 5, p=Q[0]), 0)
+        const(w("OAF"), 0)
+        const(w("FA", 0, N5, 5), 0)
+        same = (sum(sum(16 ** i for i in range(e + 1)) * 2 ** (3 - e) for e in range(4)), sum((16 - 2 ** (3 - e)) * 16 ** (3 - e) for e in range(4)))
+        for p, word in (((0, 64), same[0]), ((64, 128), same[1])):
+            act(w("IDL", p=p), w("PU", p=p), ACT.Identity, -float(word), float(word))
     for k in range(3):
         tt(v("TT", ALL, ALL, DIFF + k), v("NI", ALL, ALL, 3 - k), v("NI", ALL, ALL, 2 - k), A.subtract)
     for b in range(2):
         tt(v("TT", S(6 * b, 6 * b + 6), ALL, DIFF + 3), v("NI", S(6 * b, 6 * b + 6), ALL, 0), v("TT", S(0, 6), ALL, ADDR), A.subtract)
+    quant("Uc", "Us", "UU", 0, 128, 0)
+    scan(w("SW"), w("HR"), w("UM"))
+    gather("s", w("Ps"), w("Us"), w("LPU"))
+    op("v", lambda e: e.tensor_copy(T.Pc[:, 0:128].bitcast(dt.uint32), T.Uc[:, 0:128].bitcast(dt.uint32).indirect(T.LPU[:, 0:8])), [w("Uc"), w("LPU")], [w("Pc")])
+    copy("s", v("TT", even, ALL, WORD, p=(0, 64)), w("SW", 3, 96, 4, p=(0, 64)))
+    act(v("TT", even, ALL, WORD, p=(64, 128)), w("SW", 3, 96, 4, p=(64, 128)), ACT.Identity, -1.0, 16.0 * sum(16 ** e for e in range(4)))
+    copy("s", v("TT", odd, ALL, WORD), w("SW", 99, 192, 4))
+    later()
     quant_x(0, 0)
+    send_x(0, 0, NO)
     sa = score(0, 0)
+    for first, rows in ((0, S(0, ADDR)), (1, S(WORD, ADDR))):
+        one, zero = v("TT", S(6 + first, 12, 2), ALL, rows), v("TT", S(first, 6, 2), ALL, rows)
+        tt(one, one, zero, A.subtract)
+    up = v("TT", S(0, 6), ALL, S(DIFF, ADDR + 1))
+    act(up, up, ACT.Identity, 1.0, UP)
     quant_x(0, 1)
     sb = score(0, 1)
-    send_x(0, 0, C, 0)
-    scan(w("SW"), w("HR"), w("UM"))
-    scan(w("SF", p=Q[0]), w("HR", 0, 96, p=Q[0]), w("UF", p=Q[0]))
-    const(w("D0", 0, 768, 2), 0)
+    send_x(0, NO, C)
     bits(sa, 0)
-    copy("v", v("TT", even, ALL, WORD), w("SW", 3, 96, 4))
-    copy("v", v("TT", odd, ALL, WORD), w("SW", 99, 192, 4))
-    copy("v", v("TT", even, ALL, FIRST, p=Q[0]), w("SF", 3, 96, 4, p=Q[0]))
     edges(0)
-    bits(sb, 1)
-    edges(1)
-    for r, p in ((S(0, ADDR), (0, 128)), (FIRST, Q[0])):
-        tt(v("TT", S(6, 12), ALL, r, p=p), v("TT", S(6, 12), ALL, r, p=p), v("TT", S(0, 6), ALL, r, p=p), A.subtract)
-    for ph in range(4):
-        turn(w("D1", 2 * ph + 1, 768, 8), v("TT", S(0, 6), ph))
     for ph in range(4):
         turn(w("D0", 2 * ph + 1, 768, 8), v("TT", S(6, 12), ph))
-    for half in range(2):
-        ts(w("L2", half, 2 * LC, 2), w("ALI"), 2.0, A.mult)
-    copy("v", w("PU"), w("PUI"))
+    bits(sb, 1)
+    edges(1)
+    latest()
+    for ph in range(4):
+        turn(w("D1", 2 * ph + 1, 768, 8), v("TT", S(0, 6), ph))
+    quant_ct(2)
     choose(0, C)
-    turn_edges(0)
-    const(w("FA", p=Q[1]), 2)
-    const(w("FA", p=Q[3]), 16)
-    const(w("GG", 0, N5, 5), 0)
-    const(w("Y5", 4, N5, 5), 0)
-    const(w("OAF"), 0)
-    const(w("FA", 0, N5, 5), 0)
-    same = (sum(sum(16 ** i for i in range(e + 1)) * 2 ** (3 - e) for e in range(4)), sum((2 ** (e + 1) - 1) * 16 ** (3 - e) for e in range(4)))
-    for p, word in (((0, 64), same[0]), ((64, 128), same[1])):
-        act(w("IDL", p=p), w("PU", p=p), ACT.Identity, -float(word), float(word))
+    quant_ct(3)
 
-    def unpack(src, dst, banks, qs):
-        outs = [product(banks[b], [("CTc", "CTs", 128 * b)], src, 0, C) for b in range(4)]
-        return [(qs[b], w(dst, 2 * C * b, 2 * C * (b + 1), 2), outs[b]) for b in range(4)]
+    def unpack(src, t, dst, banks, c0, c1, bs=range(4)):
+        q = (src + "c%d" % t, src + "s%d" % t)
+        return [(w(dst, 2 * (C * b + c0), 2 * (C * b + c1), 2), product(bank, [("CTc", "CTs", 128 * b)], q, c0, c1)) for b, bank in zip(bs, banks)]
 
     def take(jobs):
-        for q, out, ps in jobs:
-            copy(q, out, ps, 2.0 ** -6)
+        for out, ps in jobs:
+            copy("s", out, ps, 2.0 ** -6)
 
-    def carries(t, gaps):
+    def carries(t, meanwhile):
         y = lambda i, p: v("YY", i, p=p)
-        m = lambda p: w("FA", 4, N5, 5, p=p)
+        m = lambda p: w("MM", 4, N5, 5, p=p)
+        m4 = w("FA", 4, N5, 5, p=Q[3])
+        edge = lambda k: v("CE", ALL, EDGE + k, p=Q[0])
+        lift = lambda k: w("FB", k, N5, 5, p=Q[0])
         AND, SHR = A.bitwise_and, A.logical_shift_right
-
-        def through(e):
-            tt(w("Y5", e, N5, 5, p=Q[3]), w("Z5", e, N5, 5, p=Q[2]), w("WS", p=Q[3]), A.mult)
 
         def flags(src, first, step, p, ks):
             for k in ks:
                 ts(w("GG", 4 - k, N5, 5, p=p), src, first + step * k, SHR, 1, AND)
-        tt(y(0, Q[0]), v("CH", ALL, FIRST, p=Q[0]), m(Q[0]), A.mult)
         for e in range(4):
             tt(w("Y5", e, N5, 5, p=(0, 96)), v("CH", ALL, e, p=(0, 96)), v("CH", ALL, 16 + WORD, p=(0, 96)), A.mult)
         act(w("WS"), v("CH", ALL, WORD), ACT.Identity, w("PU"), w("IDL"))
-        ts(w("M1", p=Q[0]), y(0, Q[0]), WIDE, AND)
+        tt(lift(3), edge(0), edge(3), A.max)
+        tt(lift(4), edge(1), edge(4), A.mult)
+        tt(m(Q[0]), edge(2), edge(5), A.mult)
+        act(w("NS"), v("CH", ALL, S(16 + DIFF, 16 + ADDR + 1)), ACT.Identity, 1.0, -UP)
+        act(w("NE"), v("CH", ALL, S(DIFF, ADDR + 1)), ACT.Identity, 1.0, -UP)
+        copy("s", lift(1), edge(3))
+        copy("s", lift(2), edge(0))
+        ts(w("Z0", p=Q[0]), w("Y5", p=Q[0]), CLOSE >> 3, AND, A0 - 3, SHR)
         ts(w("Z5", p=(0, 96)), w("Y5", p=(0, 96)), WIDE, AND)
-        tt(y(1, Q[0]), v("CH", ALL, 16 + WORD, p=Q[0]), w("M1", p=Q[0]), A.mult)
-        through(0)
-        ts(m(Q[1]), y(1, Q[0]), CLOSE, AND, A0, SHR)
-        for e in range(1, 4):
-            through(e)
-        copy("s", w("NS"), v("CH", ALL, S(16 + DIFF, 16 + ADDR + 1)))
-        take(gaps[:1])
+        scan(w("MM", p=Q[1]), w("FB", p=Q[0]), w("Z0", p=Q[0]))
+        scan(w("YS", p=Q[1]), w("FA", p=Q[1]), w("Z5", p=Q[1]))
+        for e in range(4):
+            tt(w("Y5", e, N5, 5, p=Q[3]), w("Z5", e, N5, 5, p=Q[2]), w("WS", p=Q[3]), A.mult)
+        if t == 0:
+            waits("g", [w("EE")[1]], [])
         for k in range(4):
             p = (32 * k, 32 * k + 16)
-            copy("s", w("NS", p=p), v("CH", ALL, S(DIFF, ADDR + 1), p=p))
-        take(gaps[1:])
-        scan(w("YS", p=Q[1]), w("FA", p=Q[1]), w("Z5", p=Q[1]))
+            out, in_ = w("NS", p=p), w("NE", p=p)
+            op("g", lambda e: e.affine_select(out[0], in_[0], [[0, N5]], A.is_gt, 0.0, 1, 0), [in_], [out])
+        meanwhile()
+        tt(y(0, Q[1]), w("YS", 3, N5, 5, p=Q[1]), m(Q[1]), A.mult)
+        tt(y(1, (0, 64)), w("WS", p=(0, 64)), m((0, 64)), A.mult)
         ts(w("Z5", p=Q[3]), w("Y5", p=Q[3]), CLOSE, AND, A0, SHR)
-        tt(y(2, (0, 64)), w("WS", p=(0, 64)), m((0, 64)), A.mult)
-        ts(m(Q[3]), w("YS", 4, N5, 5, p=Q[1]), WIDE << 3, AND, 3, SHR)
-        flags(y(2, (0, 64)), B0, 4, (0, 64), range(3))
+        ts(m4, y(0, Q[1]), WIDE << 3, AND, 3, SHR)
+        flags(y(1, (0, 64)), B0, 4, (0, 64), (0, 1))
         scan(w("YS", p=Q[3]), w("FA", p=Q[3]), w("Z5", p=Q[3]))
-        tt(w("YS", 4, N5, 5, p=Q[2]), w("WS", p=Q[2]), m(Q[3]), A.mult)
-        flags(y(2, (0, 64)), B0, 4, (0, 64), (3,))
-        flags(w("YS", 4, N5, 5, p=(64, 128)), A0, 1, (64, 128), range(4))
+        tt(w("YS", 4, N5, 5, p=Q[2]), w("WS", p=Q[2]), m4, A.mult)
+        flags(y(1, (0, 64)), B0, 4, (0, 64), (2, 3))
+        flags(w("YS", 4, N5, 5, p=(64, 128)), A0 + 3, -1, (64, 128), range(4))
         scan(w("XS"), w("GG"), w("NS"))
         ts(w("LA%d" % t), w("XS", 4, 5 * LC, 5), 2.0, A.mult)
         send(w("LR%d" % t), w("LA%d" % t, LO, LC), "l%d" % t)
@@ -403,52 +433,65 @@ def rank_program(g, core, T, topo):
 
     for t in range(ROUNDS):
         last = t + 1 == ROUNDS
-        fo = unpack(("Qc%d" % t, "Qs%d" % t), "FO", (2, 3, 0, 4), "ssss")
+        fo = fo + unpack("Q", t, "FO", (6, 7, 0, 2), NO, C) if t else unpack("Q", t, "FO", (2, 3, 4, 5), 0, C)
         for q, a, b in PICKS:
             gather(q, w("RD", 32 * a, 32 * b), w("TW", 8, 776), w("L2", 2 * a, 2 * b))
         turn_edges(1)
         for q, a, b in PICKS:
             turn(v("CH", S(a, b)), w("RD", 32 * a, 32 * b))
-            if q == "v":
-                tt(w("FA", 4, N5, 5, p=Q[0]), v("CE", ALL, EDGE, p=Q[0]), v("CE", ALL, EDGE + 1, p=Q[0]), A.mult)
-        take(fo[:2])
-        fp = unpack(("Ac%d" % t, "As%d" % t), "FP", (1, 5, 6, 7), "sssv")
-        carries(t, fo[2:] + fp[:3])
+        turn_edges(0)
+        if t == 0:
+            load("y", "Wc", T.wc[:], after=[v("CH")])
+            load("y", "Ws", T.ws[:])
+        if t == 1:
+            load("y", "VB", T.v[:], after=[v("CH")])
+        take(fo[:2] if t else fo[:1])
+        fp = unpack("A", t, "FP", (1, 3, 4, 5) if t else (1, 0, 6, 7), 0, NO)
+
+        def meanwhile():
+            take(fo[2:] if t else fo[1:])
+            fp.extend(unpack("A", t, "FP", (0, 2, 6, 7) if t else (2, 3, 4, 5), NO, C))
+            take(fp[:6])
+        carries(t, meanwhile)
         for b in range(4):
             gather("vsvs"[b], w("ZO", b, 4 * NO, 4), w("FO", 2 * C * b, 2 * C * (b + 1)), w("LA%d" % t, 0, LO))
+        take(fp[6:])
         quant("ZOc", "ZOs", "ZO", 0, NO, 0)
         outs = layer(0)
-        take(fp[3:])
+
         for b in range(4):
             gather("svsv"[b], w("ZR", b, 4 * NR, 4), w("FP", 2 * C * b, 2 * C * (b + 1)), w("LR%d" % t))
         quant("ZRc", "ZRs", "ZR", 0, NR, 0)
-        if t == 0:
+        if t == 1:
             quant("Vc", "Vs", "VB", 0, 128, 0)
         if not last:
             for half in range(2):
                 copy("v", w("L2", 2 * LO + half, 2 * LC, 2), w("LR%d" % t))
         if last:
             addresses_out()
-        state(0, outs, "ssss")
+        state(0, outs, "ssvs")
         quant_x(t + 1, 0)
         if last:
             outs2 = layer(1)
             state(1, outs2, "vsvs")
             quant_x(t + 1, 1)
         else:
-            send_x(t + 1, 0, NO, 0)
+            send_x(t + 1, 0, NO)
             outs2 = layer(1)
             sa = score(t + 1, 0)
-            state(1, outs2, "ssss")
+            state(1, outs2, "ssvs")
+            fo = unpack("Q", t + 1, "FO", (2, 3, 4, 5), 0, NO)
             bits(sa, 0)
             quant_x(t + 1, 1)
+            take(fo[:2])
+            fo = fo[2:]
             edges(0)
-            send_x(t + 1, NO, C, 1)
+            send_x(t + 1, NO, C)
             sb = score(t + 1, 1)
-            choose(0, NO)
+            choose(0, EARLY)
             bits(sb, 1)
             edges(1)
-            turn_edges(0)
+            choose(EARLY, NO)
             choose(NO, C)
 
     qc, qs = "Qc%d" % ROUNDS, "Qs%d" % ROUNDS

import math
import numpy as np
from concourse.mybir import dt, AluOpType, ActivationFunctionType

CODES = "float8_e4m3fn_x4"
C, NO, NR, ROUNDS = 384, 224, 160, 3
PARTS = ((0, NO), (NO, C))
LC, LO = C // 16, NO // 16
A0, B0 = 15, 3
CLOSE = sum(2 ** (A0 + k) for k in range(4))
WIDE = sum(2 ** (B0 + 4 * k) for k in range(4))
WORD, DIFF, ADDR, EDGE = 4, 5, 9, 10
N5 = 5 * LC
UP = 512.0
LIFT = 32.0
EDGE_ROWS = ((-LIFT, LIFT), ((LIFT ** 2 - 1) / LIFT ** 3, 1 / LIFT ** 3), (3.0, 1.0), (-LIFT, LIFT), (LIFT - 1, 1.0), (1.0, 1.0))
LN2 = math.log(2.0)
ONE_CLOSE = (math.log(2.03), math.log(1.005 / 2.03))
ONE_WIDE = (4 * LN2, -4 * LN2 + 3e-5)
ALL_WIDE = (4 * LN2, math.log(1 / 15))
NOT_CLOSE = (-LN2, 4 * LN2 + 3e-5)

_F, _I, _B, _U = "float32", "int32", "bfloat16", "uint16"
SCRATCH = {
    "NX": ("sbuf", [128, 192], _I), "NT": ("sbuf", [128, 12, 4, 4], _I), "CI": ("sbuf", [128, 12, 4, 4], _I), "NI": ("sbuf", [128, 12, 4, 4], _I),
    "UM": ("sbuf", [128, 192], _I), "SW": ("sbuf", [128, 192], _F), "HR": ("sbuf", [128, 192], _I), "XP": ("sbuf", [128, 8], _F),
    "TT": ("sbuf", [128, 12, 4, 16], _I), "ZZ": ("sbuf", [128, 192], _F),
    "D0": ("sbuf", [128, 768], _I), "D1": ("sbuf", [128, 768], _I), "TW": ("sbuf", [128, 776], _F),
    "RD": ("sbuf", [128, 2 * C], _U), "CH": ("sbuf", [128, LC, 32], _U), "NE": ("sbuf", [128, N5], _F),
    "ED": ("sbuf", [128, LC, 2, 16], _B), "CE": ("sbuf", [128, LC, 32], _B),
    "YY": ("sbuf", [128, 2, LC], _I), "Z0": ("sbuf", [128, N5], _I), "FB": ("sbuf", [128, N5], _F), "MM": ("sbuf", [128, N5], _I),
    "Y5": ("sbuf", [128, N5], _I), "Z5": ("sbuf", [128, N5], _I), "YS": ("sbuf", [128, N5], _I), "FA": ("sbuf", [128, N5], _I),
    "WS": ("sbuf", [128, LC], _F), "GG": ("sbuf", [128, N5], _I), "NS": ("sbuf", [128, N5], _F), "XS": ("sbuf", [128, N5], _F),
    "PI": ("sbuf", [128, 1], _I), "P15": ("sbuf", [128, 1], _I), "PUI": ("sbuf", [128, 1], _I), "PU": ("sbuf", [128, 1], _F),
    "IDL": ("sbuf", [128, 1], _F), "EE": ("sbuf", [128, 2], _F), "PE": ("sbuf", [128, 2], _I),
    "LP": ("sbuf", [128, 8], _I), "LPU": ("sbuf", [128, 8], _U),
    "ALI": ("sbuf", [128, LC], _I), "L2": ("sbuf", [128, 2 * LC], _U), "OAF": ("sbuf", [128, 32], _F), "OAT": ("sbuf", [128, 32], _F),
    "CT": ("sbuf", [128, 516], _B), "CTc": ("sbuf", [128, 512], CODES), "CTs": ("sbuf", [128, 512], "uint8"),
    "UU": ("sbuf", [128, 512], _B), "Uc": ("sbuf", [128, 128], CODES), "Us": ("sbuf", [128, 128], "uint8"),
    "Pc": ("sbuf", [128, 128], CODES), "Ps": ("sbuf", [128, 128], "uint8"),
    "VB": ("sbuf", [128, 512], _B), "Vc": ("sbuf", [128, 128], CODES), "Vs": ("sbuf", [128, 128], "uint8"),
    "Wc": ("sbuf", [128, 512], CODES), "Ws": ("sbuf", [128, 512], "uint8"),
    "X": ("sbuf", [128, 4 * C], _B), "FO": ("sbuf", [128, 8 * C], _B), "FP": ("sbuf", [128, 8 * C], _B),
    "ZO": ("sbuf", [128, 4 * NO], _B), "ZR": ("sbuf", [128, 4 * NR], _B),
    "ZOc": ("sbuf", [128, NO], CODES), "ZOs": ("sbuf", [128, NO], "uint8"),
    "ZRc": ("sbuf", [128, NR], CODES), "ZRs": ("sbuf", [128, NR], "uint8"),
    "Y": ("sbuf", [128, C], _F),
}
for _t in range(ROUNDS + 1):
    SCRATCH["Qc%d" % _t] = ("sbuf", [128, C], CODES)
    SCRATCH["Qs%d" % _t] = ("sbuf", [128, C], "uint8")
for _t in range(ROUNDS):
    SCRATCH["Ac%d" % _t] = ("sbuf", [128, C], CODES)
    SCRATCH["As%d" % _t] = ("sbuf", [128, C], "uint8")
    SCRATCH["LA%d" % _t] = ("sbuf", [128, LC], _U)
    SCRATCH["LR%d" % _t] = ("sbuf", [128, LC - LO], _U)
for _t in range(8):
    SCRATCH["pb%d" % _t] = ("psum", [128, 512], _F)
SEMAPHORES = ["cv", "cs", "ct", "cg", "sent"] + ["d%d" % i for i in range(32)] + ["q%d%d" % (t, h) for t in range(ROUNDS) for h in range(2)] + ["l%d" % t for t in range(ROUNDS)]
PICKS = (("v", 0, 10), ("s", 10, 17), ("s", 17, 24))
EARLY = 176
S = slice
ALL = slice(None)


def rank_program(g, core, T, topo):
    rank = T.rank_of(core)
    if rank is None:
        return
    n = len(T.cores)
    nxt, prv = T.cores[(rank + 1) % n], T.cores[(rank - 1) % n]
    n_in = len(topo.engines(prv, core))
    rid, pid = topo.addr(nxt)[0], topo.addr(nxt)[1]
    A = AluOpType
    ACT = ActivationFunctionType
    queue = {"v": g.vector, "s": g.scalar, "t": g.tensor, "g": g, "y": g.sync}
    count, hist, waited = {}, {}, {}
    known = {q: {} for q in queue}
    behind = {}

    def v(name, *idx, p=(0, 128)):
        shape = T[name].shape
        idx = idx + (ALL,) * (len(shape) - 1 - len(idx))
        hit = np.zeros(shape[1:], bool)
        hit[idx] = True
        bits = int.from_bytes(np.packbits(hit.reshape(-1)).tobytes(), "big")
        return (T[name][(S(p[0], p[1]),) + idx], (name, p[0], p[1], bits))

    def w(name, a=0, b=None, step=1, p=(0, 128)):
        return v(name, S(a, T[name].shape[1] if b is None else b, step), p=p)

    def waits(q, reads, writes):
        need = {}
        for kind, places in (("r", reads), ("w", writes)):
            for r in places:
                bank = r[0].startswith("pb")
                for hk, hq, hsem, hval, hr in hist.get(r[0], []):
                    if kind == "r" and hk == "r" and not (bank and hq != q):
                        continue
                    if bank and hq == q == "t":
                        continue
                    if bank or (r[1] < hr[2] and hr[1] < r[2] and r[3] & hr[3]):
                        need[hsem] = max(need.get(hsem, 0), hval)
        for s in sorted(need, key=lambda s: s == "c" + q):
            if known[q].get(s, 0) < need[s]:
                queue[q].wait_ge(T.sem[s], need[s])
                waited[s] = max(waited.get(s, 0), need[s])
                known[q][s] = need[s]
                for s2, k in behind.get((s, need[s]), {}).items():
                    known[q][s2] = max(known[q].get(s2, 0), k)

    def note(q, sem, val, reads, writes):
        behind[(sem, val)] = dict(known[q])
        for kind, places in (("r", reads), ("w", writes)):
            for r in places:
                hist.setdefault(r[0], []).append((kind, q, sem, val, r))

    def op(q, call, reads, writes):
        reads = [a[1] for a in reads if isinstance(a, tuple)]
        writes = [a[1] for a in writes]
        waits(q, reads, writes)
        sem = "c" + q
        count[sem] = count.get(sem, 0) + 1
        call(queue[q]).then_inc(T.sem[sem], 1)
        note(q, sem, count[sem], reads, writes)

    n_dma = [0]

    def dma(q, out, in_, reads=(), writes=()):
        reads, writes = [a[1] for a in reads], [a[1] for a in writes]
        waits(q, reads, writes)
        sem = "d%d" % n_dma[0]
        n_dma[0] += 1
        count[sem] = 16
        queue[q].dma_start(out, in_).then_inc(T.sem[sem], 16)
        note(q, sem, 16, reads, writes)

    def load(q, name, src, c0=0, c1=None, after=()):
        d = w(name, c0, c1)
        dma(q, d[0].bitcast(dt.uint8) if name == "Wc" else d[0], src, after, [d])

    def lands(place, sem, val):
        hist.setdefault(place[1][0], []).append(("w", "far", sem, val, place[1]))
        count[sem] = max(count.get(sem, 0), val)

    def send(out, in_, sem, codes=False):
        waits("g", [in_[1]], [])
        count["sent"] = count.get("sent", 0) + len(topo.engines(core, nxt))
        a, b = (out[0].bitcast(dt.uint8), in_[0].bitcast(dt.uint8)) if codes else (out[0], in_[0])
        g.remote_dma(a, b, T.sem[sem], T.sem.sent, pid, rid, topo.mask(core, nxt))

    def ap(a):
        return a[0] if isinstance(a, tuple) else a

    def fill(out, val):
        op("v", lambda e: e.memset(out[0], val), [], [out])

    def act(out, in_, func=ACT.Copy, scale=1.0, bias=0.0):
        op("s", lambda e: e.activation(out[0], in_[0], func, bias=ap(bias), scale=ap(scale)), [in_, scale, bias], [out])

    def const(out, val):
        k = int(np.prod(out[0].shape[1:]))
        act(out, w("ZZ", 0, k, p=out[1][1:3]), ACT.Identity if val else ACT.Copy, 1.0, float(val))

    def copy(q, out, in_, scale=None):
        if q == "s":
            act(out, in_, ACT.Copy, 1.0 if scale is None else scale)
        elif scale is None:
            op(q, lambda e: e.tensor_copy(out[0], in_[0]), [in_], [out])
        else:
            ts(out, in_, scale, A.mult)

    def ts(out, in_, s1, o1, s2=None, o2=None):
        if o2 is None:
            op("v", lambda e: e.tensor_scalar(out[0], in_[0], ap(s1), None, o1), [in_, s1], [out])
        else:
            op("v", lambda e: e.tensor_scalar(out[0], in_[0], ap(s1), ap(s2), o1, o2), [in_, s1, s2], [out])

    def tt(out, a, b, o):
        op("v", lambda e: e.tensor_tensor(out[0], a[0], b[0], o), [a, b], [out])

    def scan(out, a, b):
        op("v", lambda e: e.tensor_tensor_scan(out[0], a[0], b[0], 0.0, A.mult, A.add), [a, b], [out])

    def turn(out, in_):
        op("v", lambda e: e.transpose(out[0], in_[0]), [in_], [out])

    def gather(q, out, win, off):
        src = win[0].indirect(off[0])
        if q == "s":
            op(q, lambda e: e.activation(out[0], src, ACT.Copy), [win, off], [out])
        else:
            op(q, lambda e: e.tensor_copy(out[0], src), [win, off], [out])

    def quant(c, s, tile, c0, c1, t0):
        qc, qs, x = w(c, c0, c1), w(s, c0, c1), w(tile, t0, t0 + 4 * (c1 - c0))
        op("v", lambda e: e.quantize_mx(qc[0], qs[0], x[0]), [x], [qc, qs])

    def product(bank, pairs, rhs, c0, c1):
        out = w("pb%d" % bank, 0, c1 - c0)
        rc, rs = w(rhs[0], c0, c1), w(rhs[1], c0, c1)
        for i, (c, s, a) in enumerate(pairs):
            lc, ls = w(c, a, a + 128), w(s, a, a + 128)
            first, last = i == 0, i == len(pairs) - 1
            op("t", lambda e: e.matmul_mx(out[0], lc[0], ls[0], rc[0], rs[0], first, last), [lc, ls, rc, rs], [out])
        return out

    def iota(out, pattern, base, mult, loose=False):
        if loose:
            op("g", lambda e: e.iota(out[0], pattern, base, mult, allow_small_or_imprecise_dtypes=True), [], [out])
        else:
            op("g", lambda e: e.iota(out[0], pattern, base, mult), [], [out])

    def mark(d, pattern, val, base):
        op("g", lambda e: e.affine_select(d[0], d[0], pattern, A.not_equal, val, base, 1), [d], [d])

    for t in range(ROUNDS):
        for h, (c0, c1) in enumerate(PARTS):
            for name in ("Ac%d" % t, "As%d" % t):
                lands(w(name, c0, c1), "q%d%d" % (t, h), 2 * n_in)
        lands(w("LR%d" % t), "l%d" % t, n_in)
    Q = [(32 * k, 32 * k + 32) for k in range(4)]

    load("y", "NX", T.nx[:])
    load("s", "ALI", T.al[:])
    load("y", "UU", T.u[:])
    load("y", "X", T.x[:, 0:4 * NO], 0, 4 * NO)
    load("y", "X", T.x[:, 4 * NO:4 * C], 4 * NO, 4 * C)

    even, odd = S(0, 12, 2), S(1, 12, 2)
    fill(w("ZZ"), 0.0)
    fill(w("CT"), 0.0)
    fill(w("EE"), 1.0)
    iota(w("PI"), [[1, 1]], 0, 1)
    iota(w("LP"), [[16, 8]], 0, 0)
    mark(w("CT", 3, 515, 4), [[-1, 128]], 64.0, 0)
    iota(v("TT", S(0, 6), ALL, ADDR), [[128, 3], [0, 2], [1, 4]], 0, 4)
    for k, row in enumerate(EDGE_ROWS):
        for c in range(2):
            if row[c] != 1.0:
                mark(w("EE", c, c + 1), [[0, 1]], row[c], -(EDGE + k))
    act(w("HR"), w("ZZ"), ACT.Exp, 1.0, LN2 + 3e-5)
    for k in range(1, 4):
        a = v("TT", S(0, 6), ALL, ADDR, p=Q[k])
        act(a, a, ACT.Identity, 1.0, -128.0 * k)
    const(w("HR", 0, 96, p=(64, 128)), 16)
    const(w("HR", 96, 192, p=Q[0]), 16)

    def quant_ct(b):
        quant("CTc", "CTs", "CT", 128 * b, 128 * b + 128, 3 - b)
    ts(w("P15"), w("PI"), 15, A.bitwise_and)
    ts(w("PE", 0, 1), w("PI"), 32.0, A.is_ge)
    ts(w("PUI"), w("PI"), 4, A.logical_shift_right, 1, A.bitwise_and)
    ts(w("PE", 1, 2), w("P15"), EDGE + 3.0, A.is_ge, 16.0, A.mult)
    ts(w("LP", 0, 1), w("P15"), float(EDGE), A.is_ge)
    for k, (low, high) in enumerate(((ONE_CLOSE, ONE_WIDE), (ONE_WIDE, ONE_CLOSE))):
        for i in range(2):
            ts(w("XP", 2 * k + i, 2 * k + i + 1), w("PE", 0, 1), high[i] - low[i], A.mult, low[i], A.add)
    tt(w("LP", 0, 1), w("LP", 0, 1), w("PE", 1, 2), A.add)
    copy("v", w("PU"), w("PUI"))
    quant_ct(0)
    copy("v", w("LPU"), w("LP"))
    for half in range(2):
        ts(w("L2", half, 2 * LC, 2), w("ALI"), 2.0, A.mult)

    def send_x(t, c0, c1):
        send(w("Ac%d" % t, c0, c1), w("Qc%d" % t, c0, c1), "q%d%d" % (t, c0 > 0), True)
        send(w("As%d" % t, c0, c1), w("Qs%d" % t, c0, c1), "q%d%d" % (t, c0 > 0))

    def quant_x(t, h):
        c0, c1 = PARTS[h]
        quant("Qc%d" % t, "Qs%d" % t, "X", c0, c1, 4 * c0)

    def score(t, h):
        c0, c1 = PARTS[h]
        return product(h, [("Pc", "Ps", 0)], ("Qc%d" % t, "Qs%d" % t), c0, c1)

    def bits(ps, h):
        c0, c1 = PARTS[h]
        ts(w("D1", 2 * c0, 2 * c1, 2), ps, 0.0, A.is_gt)

    def edges(h):
        c0, c1 = PARTS[h]
        for half in range(2):
            act(v("ED", S(c0 // 16, c1 // 16), half, p=Q[0]), w("D1", 2 * c0, 2 * c1, 2, p=Q[0]), ACT.Identity, w("EE", 0, 1, p=Q[0]), w("EE", 1, 2, p=Q[0]))

    def turn_edges(h):
        c = S(PARTS[h][0] // 16, PARTS[h][1] // 16)
        turn(v("CE", c, p=Q[0]), v("ED", c, p=Q[0]))

    def choose(c0, c1):
        scan(w("TW", 7 + 2 * c0, 7 + 2 * c1), w("D0", 2 * c0, 2 * c1), w("D1", 2 * c0, 2 * c1))

    turn(v("NT"), w("NX"))
    quant_ct(1)
    ts(v("CI"), v("NT"), 9, A.logical_shift_right)
    ts(v("NI"), v("NT"), 511, A.bitwise_and)
    for p, (scale, bias) in (((0, 64), ALL_WIDE), ((64, 128), NOT_CLOSE)):
        act(w("UM", 0, 96, p=p), v("CI", even, p=p), ACT.Exp, scale, bias)
    const(w("HR", 0, 192, 4), 0)
    for k, (out, half) in enumerate(((w("UM", 96, 192), odd), (v("TT", even, ALL, S(0, 4)), even))):
        act(out, v("CI", half), ACT.Exp, w("XP", 2 * k, 2 * k + 1), w("XP", 2 * k + 1, 2 * k + 2))

    def later():
        const(v("TT", odd, ALL, S(0, 4)), 0)
        const(v("TT", S(6, 12), ALL, ADDR), 0)
        for b in range(2):
            const(v("TT", S(6 * b, 6 * b + 6), ALL, S(EDGE, 16)), 0)
        for b in range(2):
            const(w("D0", C * b, C * b + C, 2), 0)

    def latest():
        const(w("FA", p=Q[1]), 2)
        const(w("FA", p=Q[3]), 16)
        const(w("GG", 0, N5, 5), 0)
        const(w("Y5", 4, N5, 5), 0)
        const(w("FB", 0, N5, 5, p=Q[0]), 0)
        const(w("OAF"), 0)
        const(w("FA", 0, N5, 5), 0)
        same = (sum(sum(16 ** i for i in range(e + 1)) * 2 ** (3 - e) for e in range(4)), sum((16 - 2 ** (3 - e)) * 16 ** (3 - e) for e in range(4)))
        for p, word in (((0, 64), same[0]), ((64, 128), same[1])):
            act(w("IDL", p=p), w("PU", p=p), ACT.Identity, -float(word), float(word))
    for k in range(3):
        tt(v("TT", ALL, ALL, DIFF + k), v("NI", ALL, ALL, 3 - k), v("NI", ALL, ALL, 2 - k), A.subtract)
    for b in range(2):
        tt(v("TT", S(6 * b, 6 * b + 6), ALL, DIFF + 3), v("NI", S(6 * b, 6 * b + 6), ALL, 0), v("TT", S(0, 6), ALL, ADDR), A.subtract)
    quant("Uc", "Us", "UU", 0, 128, 0)
    scan(w("SW"), w("HR"), w("UM"))
    gather("s", w("Ps"), w("Us"), w("LPU"))
    op("v", lambda e: e.tensor_copy(T.Pc[:, 0:128].bitcast(dt.uint32), T.Uc[:, 0:128].bitcast(dt.uint32).indirect(T.LPU[:, 0:8])), [w("Uc"), w("LPU")], [w("Pc")])
    copy("s", v("TT", even, ALL, WORD, p=(0, 64)), w("SW", 3, 96, 4, p=(0, 64)))
    act(v("TT", even, ALL, WORD, p=(64, 128)), w("SW", 3, 96, 4, p=(64, 128)), ACT.Identity, -1.0, 16.0 * sum(16 ** e for e in range(4)))
    copy("s", v("TT", odd, ALL, WORD), w("SW", 99, 192, 4))
    later()
    quant_x(0, 0)
    send_x(0, 0, NO)
    sa = score(0, 0)
    for first, rows in ((0, S(0, ADDR)), (1, S(WORD, ADDR))):
        one, zero = v("TT", S(6 + first, 12, 2), ALL, rows), v("TT", S(first, 6, 2), ALL, rows)
        tt(one, one, zero, A.subtract)
    up = v("TT", S(0, 6), ALL, S(DIFF, ADDR + 1))
    act(up, up, ACT.Identity, 1.0, UP)
    quant_x(0, 1)
    sb = score(0, 1)
    send_x(0, NO, C)
    bits(sa, 0)
    edges(0)
    for ph in range(4):
        turn(w("D0", 2 * ph + 1, 768, 8), v("TT", S(6, 12), ph))
    bits(sb, 1)
    edges(1)
    latest()
    for ph in range(4):
        turn(w("D1", 2 * ph + 1, 768, 8), v("TT", S(0, 6), ph))
    quant_ct(2)
    choose(0, C)
    quant_ct(3)

    def unpack(src, t, dst, banks, c0, c1, bs=range(4)):
        q = (src + "c%d" % t, src + "s%d" % t)
        return [(w(dst, 2 * (C * b + c0), 2 * (C * b + c1), 2), product(bank, [("CTc", "CTs", 128 * b)], q, c0, c1)) for b, bank in zip(bs, banks)]

    def take(jobs):
        for out, ps in jobs:
            copy("s", out, ps, 2.0 ** -6)

    def carries(t, meanwhile):
        y = lambda i, p: v("YY", i, p=p)
        m = lambda p: w("MM", 4, N5, 5, p=p)
        m4 = w("FA", 4, N5, 5, p=Q[3])
        edge = lambda k: v("CE", ALL, EDGE + k, p=Q[0])
        lift = lambda k: w("FB", k, N5, 5, p=Q[0])
        AND, SHR = A.bitwise_and, A.logical_shift_right

        def flags(src, first, step, p, ks):
            for k in ks:
                ts(w("GG", 4 - k, N5, 5, p=p), src, first + step * k, SHR, 1, AND)
        for e in range(4):
            tt(w("Y5", e, N5, 5, p=(0, 96)), v("CH", ALL, e, p=(0, 96)), v("CH", ALL, 16 + WORD, p=(0, 96)), A.mult)
        act(w("WS"), v("CH", ALL, WORD), ACT.Identity, w("PU"), w("IDL"))
        tt(lift(3), edge(0), edge(3), A.max)
        tt(lift(4), edge(1), edge(4), A.mult)
        tt(m(Q[0]), edge(2), edge(5), A.mult)
        act(w("NS"), v("CH", ALL, S(16 + DIFF, 16 + ADDR + 1)), ACT.Identity, 1.0, -UP)
        act(w("NE"), v("CH", ALL, S(DIFF, ADDR + 1)), ACT.Identity, 1.0, -UP)
        copy("s", lift(1), edge(3))
        copy("s", lift(2), edge(0))
        ts(w("Z0", p=Q[0]), w("Y5", p=Q[0]), CLOSE >> 3, AND, A0 - 3, SHR)
        ts(w("Z5", p=(0, 96)), w("Y5", p=(0, 96)), WIDE, AND)
        scan(w("MM", p=Q[1]), w("FB", p=Q[0]), w("Z0", p=Q[0]))
        scan(w("YS", p=Q[1]), w("FA", p=Q[1]), w("Z5", p=Q[1]))
        for e in range(4):
            tt(w("Y5", e, N5, 5, p=Q[3]), w("Z5", e, N5, 5, p=Q[2]), w("WS", p=Q[3]), A.mult)
        if t == 0:
            waits("g", [w("EE")[1]], [])
        for k in range(4):
            p = (32 * k, 32 * k + 16)
            out, in_ = w("NS", p=p), w("NE", p=p)
            op("g", lambda e: e.affine_select(out[0], in_[0], [[0, N5]], A.is_gt, 0.0, 1, 0), [in_], [out])
        meanwhile()
        tt(y(0, Q[1]), w("YS", 3, N5, 5, p=Q[1]), m(Q[1]), A.mult)
        tt(y(1, (0, 64)), w("WS", p=(0, 64)), m((0, 64)), A.mult)
        ts(w("Z5", p=Q[3]), w("Y5", p=Q[3]), CLOSE, AND, A0, SHR)
        ts(m4, y(0, Q[1]), WIDE << 3, AND, 3, SHR)
        flags(y(1, (0, 64)), B0, 4, (0, 64), (0, 1))
        scan(w("YS", p=Q[3]), w("FA", p=Q[3]), w("Z5", p=Q[3]))
        tt(w("YS", 4, N5, 5, p=Q[2]), w("WS", p=Q[2]), m4, A.mult)
        flags(y(1, (0, 64)), B0, 4, (0, 64), (2, 3))
        flags(w("YS", 4, N5, 5, p=(64, 128)), A0 + 3, -1, (64, 128), range(4))
        scan(w("XS"), w("GG"), w("NS"))
        ts(w("LA%d" % t), w("XS", 4, 5 * LC, 5), 2.0, A.mult)
        send(w("LR%d" % t), w("LA%d" % t, LO, LC), "l%d" % t)
        if t + 1 < ROUNDS:
            for half in range(2):
                ts(w("L2", half, 2 * LO, 2), w("XS", 4, 5 * LO, 5), 2.0, A.mult)

    def layer(h, bs=range(4)):
        z = (("ZOc", "ZOs"), ("ZRc", "ZRs"))[h]
        return [product(4 * h + b, [("Wc", "Ws", 128 * b), ("CTc", "CTs", 128 * b)], z, 0, (NO, NR)[h]) for b in bs]

    def state(h, outs, qs, bs=range(4)):
        c0, c1 = PARTS[h]
        for b in bs:
            copy(qs[b], w("X", 4 * c0 + b, 4 * c1, 4), outs[b], 2.0 ** -6)

    def addresses_out():
        copy("v", w("OAF", 0, LO), w("XS", 4, 5 * LO, 5))
        copy("v", w("OAF", LO, LC), w("LR%d" % (ROUNDS - 1)), 0.5)
        turn(w("OAT"), w("OAF"))
        for k in range(8):
            src = w("OAT", 16 * (k % 2), 16 * (k % 2) + 16, p=(32 * (k // 2), 32 * (k // 2) + LC))
            dma("y", T.oa[k:k + 1, :], src[0], [src])

    for t in range(ROUNDS):
        last = t + 1 == ROUNDS
        fo = fo + unpack("Q", t, "FO", (6, 7, 0, 2), NO, C) if t else unpack("Q", t, "FO", (2, 3, 4, 5), 0, C)
        for q, a, b in PICKS:
            gather(q, w("RD", 32 * a, 32 * b), w("TW", 8, 776), w("L2", 2 * a, 2 * b))
        turn_edges(1)
        for q, a, b in PICKS:
            turn(v("CH", S(a, b)), w("RD", 32 * a, 32 * b))
        turn_edges(0)
        if t == 0:
            load("y", "Wc", T.wc[:], after=[v("CH")])
            load("y", "Ws", T.ws[:])
        if t == 1:
            load("y", "VB", T.v[:], after=[v("CH")])
        take(fo[:2] if t else fo[:1])
        fp = unpack("A", t, "FP", (1, 3, 4, 5) if t else (1, 0, 6, 7), 0, NO)

        def meanwhile():
            take(fo[2:] if t else fo[1:])
            fp.extend(unpack("A", t, "FP", (0, 2, 6, 7) if t else (2, 3, 4, 5), NO, C))
            take(fp[:6])
        carries(t, meanwhile)
        for b in range(4):
            gather("vsvs"[b], w("ZO", b, 4 * NO, 4), w("FO", 2 * C * b, 2 * C * (b + 1)), w("LA%d" % t, 0, LO))
        take(fp[6:])
        quant("ZOc", "ZOs", "ZO", 0, NO, 0)
        outs = layer(0)

        for b in range(4):
            gather("svsv"[b], w("ZR", b, 4 * NR, 4), w("FP", 2 * C * b, 2 * C * (b + 1)), w("LR%d" % t))
        quant("ZRc", "ZRs", "ZR", 0, NR, 0)
        if t == 1:
            quant("Vc", "Vs", "VB", 0, 128, 0)
        if not last:
            for half in range(2):
                copy("v", w("L2", 2 * LO + half, 2 * LC, 2), w("LR%d" % t))
        if last:
            addresses_out()
        state(0, outs, "ssvs")
        quant_x(t + 1, 0)
        if last:
            outs2 = layer(1)
            state(1, outs2, "vsvs")
            quant_x(t + 1, 1)
        else:
            send_x(t + 1, 0, NO)
            outs2 = layer(1)
            sa = score(t + 1, 0)
            state(1, outs2, "ssvs")
            fo = unpack("Q", t + 1, "FO", (2, 3, 4, 5), 0, NO)
            bits(sa, 0)
            quant_x(t + 1, 1)
            take(fo[:2])
            fo = fo[2:]
            edges(0)
            send_x(t + 1, NO, C)
            sb = score(t + 1, 1)
            choose(0, EARLY)
            bits(sb, 1)
            edges(1)
            choose(EARLY, NO)
            choose(NO, C)

    qc, qs = "Qc%d" % ROUNDS, "Qs%d" % ROUNDS
    for h, (c0, c1) in enumerate(PARTS):
        out = product(h, [("Vc", "Vs", 0)], (qc, qs), c0, c1)
        dma("ys"[h], T.oc[:, 4 * c0:4 * c1], T[qc][:, c0:c1].bitcast(dt.uint8), [w(qc, c0, c1)])
        copy("sv"[h], w("Y", c0, c1), out)
        dma("ys"[h], T.y[:, c0:c1], T.Y[:, c0:c1], [w("Y", c0, c1)])
    for k in range(4):
        dma("y", T.osc[4 * k:4 * k + 4, :], T[qs][32 * k:32 * k + 4, :], [w(qs)])

    for s in sorted(count):
        if waited.get(s, 0) < count[s]:
            g.wait_ge(T.sem[s], count[s])
